import numpy as np
import ml_dtypes


def mxq(x, axis, fmt="e4m3"):
    dtype, down = {"e4m3": (ml_dtypes.float8_e4m3fn, 7), "e5m2": (ml_dtypes.float8_e5m2, 14)}[fmt]
    v = np.moveaxis(np.asarray(x, np.float32).astype(ml_dtypes.bfloat16).astype(np.float64), axis, -1)
    blocks = v.reshape(v.shape[:-1] + (-1, 32))
    amax = np.abs(blocks).max(-1, keepdims=True)
    byte = np.maximum(np.where(amax > 0, np.frexp(amax)[1] - 1 + 127, 0) - down, 1)
    scale = np.exp2(byte - 127.0)
    codes = (blocks / scale).astype(np.float32).astype(dtype).astype(np.float64)
    return np.moveaxis((codes * scale).reshape(v.shape), -1, axis)


WIDE = False


def mx_kscale(k):
    if not WIDE:
        return np.ones(k)
    levels = np.array([24, -24, 12, -12, 0])
    if k % 512:
        return np.exp2(np.random.permutation(np.resize(levels, k // 32))).repeat(32)
    a = np.empty((k // 512, 16))
    for p in range(k // 512):
        a[p, :8] = np.random.permutation(np.resize(levels, 8))
        for g in range(8):
            far = levels[np.abs(levels - a[p, g]) >= 10]
            a[p, g + 8] = far[np.random.randint(len(far))]
    return np.exp2(a.ravel()).repeat(32)


def f64(x):
    return np.asarray(x).astype(np.float64)


def striped(idx):
    return np.tile(idx.reshape(-1, 16).T, (8, 1)).astype(np.uint16)


def unstriped(offs):
    return offs[:16].T.reshape(-1).astype(np.int64)


E2M1 = np.array([0.0, 0.5, 1.0, 1.5, 2.0, 3.0, 4.0, 6.0, -0.0, -0.5, -1.0, -1.5, -2.0, -3.0, -4.0, -6.0])


def pack_weight(w, fmt):
    k, n = w.shape
    w = f64(np.asarray(w, np.float32).astype(ml_dtypes.bfloat16)).reshape(k // 32, 32, n)
    amax = np.abs(w).max(1)
    if fmt == "e4m3":
        byte = np.frexp(amax)[1] - 1 + 127 - 7
    else:
        mant, ex = np.frexp(amax / 6.0)
        byte = np.where(mant > 0.5, ex, ex - 1) + 127
    byte = np.clip(np.where(amax > 0, byte, 1), 1, 254)
    scaled = (w * np.exp2(127.0 - byte)[:, None, :]).reshape(k, n).astype(np.float32)
    by_word = np.ascontiguousarray(scaled.reshape(k // 512, 128, 4, n).transpose(0, 1, 3, 2))
    if fmt == "e4m3":
        words = by_word.astype(ml_dtypes.float8_e4m3fn).view(np.uint8)
    else:
        c = by_word.astype(ml_dtypes.float4_e2m1fn).view(np.uint8) & 0xF
        words = (c[..., 0::2] | (c[..., 1::2] << 4)).reshape(k // 512, 128, 2 * n)
    return np.ascontiguousarray(words), np.ascontiguousarray(byte.astype(np.uint8).reshape(k // 512, 16, n))


def unpack_weight(words, scales, fmt):
    g, _, n = scales.shape
    words = np.ascontiguousarray(words).reshape(g, 128, n, -1)
    if fmt == "e4m3":
        vals = words.view(ml_dtypes.float8_e4m3fn).astype(np.float64)
    else:
        nib = np.empty((g, 128, n, 4), np.uint8)
        nib[..., 0::2] = words & 0xF
        nib[..., 1::2] = words >> 4
        vals = E2M1[nib]
    vals = vals * np.repeat(np.exp2(scales.astype(np.float64) - 127.0), 8, axis=1)[..., None]
    return vals.transpose(0, 1, 3, 2).reshape(g * 512, n)


def planes(y):
    n, m = y.shape
    v = y.astype(np.float32).astype(ml_dtypes.bfloat16).astype(np.float64).reshape(n // 32, 32, m)
    top = np.abs(v).max(1)
    byte = np.clip(np.where(top > 0, np.frexp(top)[1] - 1 + 127 - 7, 1), 1, 254)
    codes = (v * np.exp2(127.0 - byte)[:, None, :]).reshape(n, m).astype(np.float32).astype(ml_dtypes.float8_e4m3fn).view(np.uint8)
    words = codes.reshape(n // 512, 128, 4, m).transpose(0, 1, 3, 2)
    return np.ascontiguousarray(words), np.ascontiguousarray(byte.astype(np.uint8).reshape(n // 512, 16, m))


K, R, N, T, J = 512, 512, 512, 2048, 1024


def setup_inputs():
    n = np.random.standard_normal
    s = mx_kscale(K)[:, None]
    u = mx_kscale(R)[:, None]
    p_tab = pack_weight(n((K, T)) * s, "e4m3")
    p_wb = pack_weight(0.7 * n((K, N)) / np.sqrt(K) / s, "e2m1")
    p_dn = pack_weight(n((K, R)) / np.sqrt(K) / s * u.T, "e2m1")
    return {
        "tab_words": p_tab[0],
        "tab_scales": p_tab[1],
        "wb_words": p_wb[0],
        "wb_scales": p_wb[1],
        "dn_words": p_dn[0],
        "dn_scales": p_dn[1],
        "upw": (2.0 * n((R, N)) / np.sqrt(R) / u).astype(np.float32),
        "x0T": (n((N, T))).astype(np.float32),
        "b": (0.3 * n(N)).astype(np.float32),
        "offs": striped(np.random.permutation(T)[:J]),
    }


def reference(tab_words, tab_scales, wb_words, wb_scales, dn_words, dn_scales, upw, x0T, b, offs):
    idx = unstriped(offs)
    tab_ = unpack_weight(tab_words, tab_scales, "e4m3")[:, idx]
    wb_ = unpack_weight(wb_words, wb_scales, "e2m1")
    dn_ = unpack_weight(dn_words, dn_scales, "e2m1")
    hs = dn_.T @ tab_
    h = hs
    h_ = mxq(h, 0, "e4m3")
    upw_ = mxq(f64(upw), 0, "e4m3")
    y = wb_.T @ tab_ + upw_.T @ h_
    out_0 = f64(x0T)[:, idx] * (y + f64(b)[:, None]) + f64(x0T)[:, idx]
    return (out_0,) + planes(out_0)

@@ -1,0 +1,191 @@
+from contextlib import ExitStack
+
+import concourse.mybir as mybir
+
+K, R, N, T, J = 512, 512, 512, 2048, 1024
+FLOPS = 2 * J * (K * R + K * N + R * N)
+
+F32 = mybir.dt.float32
+BF16 = mybir.dt.bfloat16
+I32 = mybir.dt.int32
+U32 = mybir.dt.uint32
+U16 = mybir.dt.uint16
+U8 = mybir.dt.uint8
+FP8X4 = mybir.dt.float8_e4m3fn_x4
+FP4X4 = mybir.dt.float4_e2m1fn_x4
+MULT = mybir.AluOpType.mult
+ADD = mybir.AluOpType.add
+IDENT = mybir.ActivationFunctionType.Identity
+
+P = 128
+PACK = 4
+HALF = 512
+HT = 128
+
+
+def load_scale_rows(queue, plane, scales):
+    for q in range(4):
+        queue.dma_start(plane[32 * q : 32 * q + 32, :].bitcast(I32), scales[0, 4 * q : 4 * q + 4, :].bitcast(I32).partition_broadcast(8))
+
+
+def tile_list_xcross_noneP_kernel(tc, tab_words, tab_scales, wb_words, wb_scales, dn_words, dn_scales, upw, x0T, b, offs, out_0, out_1, out_2):
+    nc = tc.nc
+    with ExitStack() as ctx:
+        keep = ctx.enter_context(tc.tile_pool(name="keep", bufs=1))
+        ring = ctx.enter_context(tc.tile_pool(name="ring", bufs=2))
+        psum_h = ctx.enter_context(tc.psum_pool(name="psum_h", bufs=4))
+        psum_y = ctx.enter_context(tc.psum_pool(name="psum_y", bufs=4))
+
+        offsets = keep.tile([P, J // 16], U16, name="offsets")
+        tab_s = keep.tile([P, T], U8, name="tab_s", align_bytes=64)
+        tab_w = keep.tile([P, T], I32, name="tab_w", align_bytes=64)
+        dn_s_raw = keep.tile([P, R], U8, name="dn_s_raw", tag="reused", align_bytes=64)
+        wb_s_raw = keep.tile([P, N], U8, name="wb_s_raw", align_bytes=64)
+        dn_w_raw = keep.tile([P, 2 * R], U8, name="dn_w_raw", align_bytes=64)
+        wb_w_raw = keep.tile([P, 2 * N], U8, name="wb_w_raw", align_bytes=64)
+        up_raw = keep.tile([P, PACK, N], F32, name="up_raw", align_bytes=64)
+        bias = keep.tile([P, PACK], F32, name="bias")
+        bias1 = keep.tile([P, PACK], F32, name="bias1")
+        x0 = [keep.tile([P, T], F32, name="x0_%d" % t, align_bytes=64) for t in range(PACK)]
+
+
+        x0_rows = x0T.rearrange("(p t) c -> p t c", t=PACK)
+        nc.sync.dma_start(offsets[:], offs)
+        load_scale_rows(nc.sync, tab_s, tab_scales)
+        nc.sync.dma_start(tab_w[:], tab_words[0].rearrange("p t i -> p (t i)").bitcast(I32))
+        nc.sync.dma_start(dn_w_raw[:].bitcast(I32), dn_words[0].bitcast(I32))
+        load_scale_rows(nc.sync, dn_s_raw, dn_scales)
+        nc.sync.dma_start(up_raw[:], upw.rearrange("(p i) n -> p i n", i=PACK))
+        nc.sync.dma_start(wb_w_raw[:].bitcast(I32), wb_words[0].bitcast(I32))
+        load_scale_rows(nc.sync, wb_s_raw, wb_scales)
+        nc.sync.dma_start(bias[:], b.rearrange("(p t) -> p t", t=PACK))
+        for t in range(PACK):
+            nc.sync.dma_start(x0[t][:], x0_rows[:, t, :])
+        nc.scalar.activation(bias1[:], bias[:], IDENT, bias=1.0)
+
+        def deal(name, words_raw, scales_raw):
+            words = keep.tile([P, 2 * N], U8, name=name + "_w", align_bytes=64)
+            scales = keep.tile([P, N], U8, name=name + "_s", align_bytes=64)
+            nc.vector.tensor_copy(
+                words[:].bitcast(U16).rearrange("p (t m) -> p t m", t=PACK),
+                words_raw[:].bitcast(U16).rearrange("p (m t) -> p t m", t=PACK),
+            )
+            nc.vector.tensor_copy(
+                scales[:].rearrange("p (t m) -> p t m", t=PACK),
+                scales_raw[:].rearrange("p (m t) -> p t m", t=PACK),
+            )
+            return words, scales
+
+        halves = range(J // HALF)
+        lists = [offsets[:, h * HALF // 16 : (h + 1) * HALF // 16] for h in halves]
+        v_s = [keep.tile([P, HALF], U8, name="v_s%d" % h, align_bytes=64) for h in halves]
+        for h in halves:
+            nc.vector.tensor_copy(v_s[h][:], tab_s[:].indirect(lists[h]))
+        dn_w, dn_s = deal("dn", dn_w_raw, dn_s_raw)
+        v_w = [
+            keep.tile([P, HALF], U32, name="v_w0", tag="reused", align_bytes=64),
+            keep.tile([P, HALF], U32, name="v_w1", align_bytes=64),
+        ]
+        for h in halves:
+            nc.vector.tensor_copy(v_w[h][:], tab_w[:].bitcast(U32).indirect(lists[h]))
+        wb_w, wb_s = deal("wb", wb_w_raw, wb_s_raw)
+
+        h_bf = [keep.tile([P, HALF, PACK], BF16, name="h_bf%d" % h, align_bytes=64) for h in halves]
+        for h in halves:
+            for c in range(HALF // HT):
+                cols = slice(c * HT, (c + 1) * HT)
+                bank = psum_h.tile([P, PACK, HT], F32, name="h_bank")
+                for t in range(PACK):
+                    nc.tensor.matmul_mx(
+                        out=bank[:, t, :],
+                        lhsT=dn_w[:, 2 * P * t : 2 * P * (t + 1)].bitcast(FP4X4),
+                        lhsT_scale=dn_s[:, P * t : P * (t + 1)],
+                        rhs=v_w[h][:, cols].bitcast(FP8X4),
+                        rhs_scale=v_s[h][:, cols],
+                        start=True,
+                        stop=True,
+                    )
+                nc.scalar.copy(h_bf[h][:, cols, :], bank[:].rearrange("p t j -> p j t"))
+
+        up_bf = keep.tile([P, PACK * N], BF16, name="up_bf", align_bytes=64)
+        up_w = keep.tile([P, N], U32, name="up_w", align_bytes=64)
+        up_s = keep.tile([P, N], U8, name="up_s", align_bytes=64)
+        nc.vector.tensor_copy(
+            up_bf[:].rearrange("p (t m i) -> p m i t", t=PACK, i=PACK),
+            up_raw[:].rearrange("p i (m t) -> p m i t", t=PACK),
+        )
+        nc.vector.quantize_mx(out=up_w[:].bitcast(FP8X4), scales=up_s[:], in_=up_bf[:])
+
+        h_w = [keep.tile([P, HALF], U32, name="h_w%d" % h, align_bytes=64) for h in halves]
+        h_s = [keep.tile([P, HALF], U8, name="h_s%d" % h, align_bytes=64) for h in halves]
+        for h in halves:
+            nc.vector.quantize_mx(out=h_w[h][:].bitcast(FP8X4), scales=h_s[h][:], in_=h_bf[h][:].rearrange("p j t -> p (j t)"))
+
+        res = [keep.tile([P, PACK, HALF], F32, name="res%d" % h, align_bytes=64) for h in halves]
+        o_w = keep.tile([P, J], I32, name="o_w", align_bytes=64)
+        o_s = keep.tile([P, J], U8, name="o_s", align_bytes=64)
+        out_rows = out_0.rearrange("(p t) j -> p t j", t=PACK)
+        out_words = out_1[0].rearrange("p j i -> p (j i)").bitcast(I32)
+
+        def cross(h, t, early=False, pieces=1):
+            bank = psum_y.tile([P, HALF], F32, name="y_bank")
+            nc.tensor.matmul_mx(
+                out=bank[:],
+                lhsT=wb_w[:, 2 * P * t : 2 * P * (t + 1)].bitcast(FP4X4),
+                lhsT_scale=wb_s[:, P * t : P * (t + 1)],
+                rhs=v_w[h][:].bitcast(FP8X4),
+                rhs_scale=v_s[h][:],
+                start=True,
+                stop=False,
+            )
+            nc.tensor.matmul_mx(
+                out=bank[:],
+                lhsT=up_w[:, P * t : P * (t + 1)].bitcast(FP8X4),
+                lhsT_scale=up_s[:, P * t : P * (t + 1)],
+                rhs=h_w[h][:].bitcast(FP8X4),
+                rhs_scale=h_s[h][:],
+                start=False,
+                stop=True,
+            )
+            if early:
+                picked = keep.tile([P, HALF], F32, name="picked", align_bytes=64)
+                nc.vector.tensor_copy(picked[:], x0[t][:].indirect(lists[h]))
+                nc.vector.scalar_tensor_tensor(res[h][:, t, :], bank[:], bias1[:, t : t + 1], picked[:], ADD, MULT)
+            else:
+                y1 = ring.tile([P, HALF], F32, name="y1")
+                nc.scalar.activation(y1[:], bank[:], IDENT, bias=bias1[:, t : t + 1])
+                width = HALF // pieces
+                for c in range(pieces):
+                    cols = slice(c * width, (c + 1) * width)
+                    part = offsets[:, (h * HALF + c * width) // 16 : (h * HALF + (c + 1) * width) // 16]
+                    nc.vector.tensor_tensor(res[h][:, t, cols], x0[t][:].indirect(part), y1[:, cols], MULT)
+            nc.sync.dma_start(out_rows[:, t, h * HALF : (h + 1) * HALF], res[h][:, t, :])
+
+        def planes(h, c0, c1, copy):
+            width = c1 - c0
+            o_bf = keep.tile([P, width, PACK], BF16, name="o_bf%d_%d" % (h, c0), align_bytes=64)
+            copy(
+                o_bf[:].rearrange("p (c i) t -> p c t i", i=4),
+                res[h][:, :, c0:c1].rearrange("p t (c i) -> p c t i", i=4),
+            )
+            return o_bf
+
+        def quant(h, c0, c1, o_bf):
+            cols = slice(h * HALF + c0, h * HALF + c1)
+            nc.vector.quantize_mx(out=o_w[:, cols].bitcast(FP8X4), scales=o_s[:, cols], in_=o_bf[:].rearrange("p j t -> p (j t)"))
+            nc.sync.dma_start(out_words[:, cols], o_w[:, cols])
+
+        cross(0, 0, early=True)
+        for h, t in ((0, 1), (1, 0), (0, 2), (0, 3), (1, 1)):
+            cross(h, t)
+        cross(1, 2)
+        first = planes(0, 0, HALF, nc.scalar.copy)
+        cross(1, 3, pieces=2)
+        second = planes(1, 0, HALF // 2, nc.scalar.copy)
+        third = planes(1, HALF // 2, HALF, nc.vector.tensor_copy)
+        quant(0, 0, HALF, first)
+        quant(1, HALF // 2, HALF, third)
+        quant(1, 0, HALF // 2, second)
+        for q in range(4):
+            queue = nc.sync if q % 2 == 0 else nc.scalar
+            queue.dma_start(out_2[0, 4 * q : 4 * q + 4, :].bitcast(I32), o_s[32 * q : 32 * q + 4, :].bitcast(I32))

@@ -32,7 +32,6 @@ def tile_list_xcross_noneP_kernel(tc, tab_words, tab_scales, wb_words, wb_scales
     nc = tc.nc
     with ExitStack() as ctx:
         keep = ctx.enter_context(tc.tile_pool(name="keep", bufs=1))
-        ring = ctx.enter_context(tc.tile_pool(name="ring", bufs=2))
         psum_h = ctx.enter_context(tc.psum_pool(name="psum_h", bufs=4))
         psum_y = ctx.enter_context(tc.psum_pool(name="psum_y", bufs=4))
 
@@ -83,8 +82,8 @@ def tile_list_xcross_noneP_kernel(tc, tab_words, tab_scales, wb_words, wb_scales
             nc.vector.tensor_copy(v_s[h][:], tab_s[:].indirect(lists[h]))
         dn_w, dn_s = deal("dn", dn_w_raw, dn_s_raw)
         v_w = [
-            keep.tile([P, HALF], U32, name="v_w0", tag="reused", align_bytes=64),
-            keep.tile([P, HALF], U32, name="v_w1", align_bytes=64),
+            keep.tile([P, HALF], U32, name="v_w0", align_bytes=64),
+            keep.tile([P, HALF], U32, name="v_w1", tag="reused", align_bytes=64),
         ]
         for h in halves:
             nc.vector.tensor_copy(v_w[h][:], tab_w[:].bitcast(U32).indirect(lists[h]))
@@ -116,18 +115,21 @@ def tile_list_xcross_noneP_kernel(tc, tab_words, tab_scales, wb_words, wb_scales
         )
         nc.vector.quantize_mx(out=up_w[:].bitcast(FP8X4), scales=up_s[:], in_=up_bf[:])
 
-        h_w = [keep.tile([P, HALF], U32, name="h_w%d" % h, align_bytes=64) for h in halves]
         h_s = [keep.tile([P, HALF], U8, name="h_s%d" % h, align_bytes=64) for h in halves]
-        for h in halves:
+        h_w = {}
+
+        def quantise_h(h, tag):
+            h_w[h] = keep.tile([P, HALF], U32, name="h_w%d" % h, tag=tag, align_bytes=64)
             nc.vector.quantize_mx(out=h_w[h][:].bitcast(FP8X4), scales=h_s[h][:], in_=h_bf[h][:].rearrange("p j t -> p (j t)"))
 
-        res = [keep.tile([P, PACK, HALF], F32, name="res%d" % h, align_bytes=64) for h in halves]
+        quantise_h(0, "h_w0")
+
         o_w = keep.tile([P, J], I32, name="o_w", align_bytes=64)
         o_s = keep.tile([P, J], U8, name="o_s", align_bytes=64)
         out_rows = out_0.rearrange("(p t) j -> p t j", t=PACK)
         out_words = out_1[0].rearrange("p j i -> p (j i)").bitcast(I32)
 
-        def cross(h, t, early=False, pieces=1):
+        def product(h, t):
             bank = psum_y.tile([P, HALF], F32, name="y_bank")
             nc.tensor.matmul_mx(
                 out=bank[:],
@@ -147,45 +149,65 @@ def tile_list_xcross_noneP_kernel(tc, tab_words, tab_scales, wb_words, wb_scales
                 start=False,
                 stop=True,
             )
-            if early:
-                picked = keep.tile([P, HALF], F32, name="picked", align_bytes=64)
-                nc.vector.tensor_copy(picked[:], x0[t][:].indirect(lists[h]))
-                nc.vector.scalar_tensor_tensor(res[h][:, t, :], bank[:], bias1[:, t : t + 1], picked[:], ADD, MULT)
-            else:
-                y1 = ring.tile([P, HALF], F32, name="y1")
-                nc.scalar.activation(y1[:], bank[:], IDENT, bias=bias1[:, t : t + 1])
-                width = HALF // pieces
-                for c in range(pieces):
-                    cols = slice(c * width, (c + 1) * width)
-                    part = offsets[:, (h * HALF + c * width) // 16 : (h * HALF + (c + 1) * width) // 16]
-                    nc.vector.tensor_tensor(res[h][:, t, cols], x0[t][:].indirect(part), y1[:, cols], MULT)
-            nc.sync.dma_start(out_rows[:, t, h * HALF : (h + 1) * HALF], res[h][:, t, :])
+            return bank
 
-        def planes(h, c0, c1, copy):
-            width = c1 - c0
-            o_bf = keep.tile([P, width, PACK], BF16, name="o_bf%d_%d" % (h, c0), align_bytes=64)
-            copy(
-                o_bf[:].rearrange("p (c i) t -> p c t i", i=4),
-                res[h][:, :, c0:c1].rearrange("p t (c i) -> p c t i", i=4),
-            )
+        def biased(h, t, tag):
+            bank = product(h, t)
+            y1 = keep.tile([P, HALF], F32, name="y1_%d_%d" % (h, t), tag=tag, align_bytes=64)
+            nc.scalar.activation(y1[:], bank[:], IDENT, bias=bias1[:, t : t + 1])
+            return y1
+
+        def cross(res, y1, j0, width, t):
+            part = offsets[:, j0 // 16 : (j0 + width) // 16]
+            c0 = j0 % HALF
+            nc.vector.tensor_tensor(res[:, t, :], x0[t][:].indirect(part), y1[:, c0 : c0 + width], MULT)
+
+        def store(res, j0, width, t0, t1):
+            nc.sync.dma_start(out_rows[:, t0:t1, j0 : j0 + width], res[:, t0:t1, :])
+
+        def rounded(res, name, copy):
+            o_bf = keep.tile([P, res.shape[2], PACK], BF16, name=name, align_bytes=64)
+            copy(o_bf[:].rearrange("p (c i) t -> p c t i", i=4), res[:].rearrange("p t (c i) -> p c t i", i=4))
             return o_bf
 
-        def quant(h, c0, c1, o_bf):
-            cols = slice(h * HALF + c0, h * HALF + c1)
+        def quantise(o_bf, j0, width):
+            cols = slice(j0, j0 + width)
             nc.vector.quantize_mx(out=o_w[:, cols].bitcast(FP8X4), scales=o_s[:, cols], in_=o_bf[:].rearrange("p j t -> p (j t)"))
             nc.sync.dma_start(out_words[:, cols], o_w[:, cols])
 
-        cross(0, 0, early=True)
-        for h, t in ((0, 1), (1, 0), (0, 2), (0, 3), (1, 1)):
-            cross(h, t)
-        cross(1, 2)
-        first = planes(0, 0, HALF, nc.scalar.copy)
-        cross(1, 3, pieces=2)
-        second = planes(1, 0, HALF // 2, nc.scalar.copy)
-        third = planes(1, HALF // 2, HALF, nc.vector.tensor_copy)
-        quant(0, 0, HALF, first)
-        quant(1, HALF // 2, HALF, third)
-        quant(1, 0, HALF // 2, second)
+        QUART = HALF // 2
+        res_a = keep.tile([P, PACK, HALF], F32, name="res_a", align_bytes=64)
+        bank = product(0, 0)
+        picked = keep.tile([P, HALF], F32, name="picked", tag="picked", align_bytes=64)
+        nc.vector.tensor_copy(picked[:], x0[0][:].indirect(lists[0]))
+        nc.vector.scalar_tensor_tensor(res_a[:, 0, :], bank[:], bias1[:, 0:1], picked[:], ADD, MULT)
+        store(res_a, 0, HALF, 0, 1)
+        quantise_h(1, "picked")
+        y_a = {t: biased(0, t, "y_a%d" % t) for t in range(1, PACK)}
+        y_b = {t: biased(1, t, "y_b%d" % t) for t in range(PACK)}
+
+        cross(res_a, y_a[1], 0, HALF, 1)
+        store(res_a, 0, HALF, 1, 2)
+        res_b = keep.tile([P, PACK, QUART], F32, name="res_b", tag="y_a1", align_bytes=64)
+        for t in range(2, PACK):
+            cross(res_b, y_b[t - 2], HALF, QUART, t - 2)
+            cross(res_a, y_a[t], 0, HALF, t)
+            store(res_a, 0, HALF, t, t + 1)
+        store(res_b, HALF, QUART, 0, 2)
+        bf_a = rounded(res_a, "bf_a", nc.scalar.copy)
+        for t in range(2, PACK):
+            cross(res_b, y_b[t], HALF, QUART, t)
+        store(res_b, HALF, QUART, 2, 4)
+        bf_b = rounded(res_b, "bf_b", nc.scalar.copy)
+        res_c = keep.tile([P, PACK, QUART], F32, name="res_c", tag="y_a3", align_bytes=64)
+        for t in range(PACK):
+            cross(res_c, y_b[t], HALF + QUART, QUART, t)
+            if t % 2 == 1:
+                store(res_c, HALF + QUART, QUART, t - 1, t + 1)
+        quantise(bf_a, 0, HALF)
+        bf_c = rounded(res_c, "bf_c", nc.vector.tensor_copy)
+        quantise(bf_b, HALF, QUART)
+        quantise(bf_c, HALF + QUART, QUART)
         for q in range(4):
             queue = nc.sync if q % 2 == 0 else nc.scalar
             queue.dma_start(out_2[0, 4 * q : 4 * q + 4, :].bitcast(I32), o_s[32 * q : 32 * q + 4, :].bitcast(I32))

@@ -32,8 +32,7 @@ def tile_list_xcross_noneP_kernel(tc, tab_words, tab_scales, wb_words, wb_scales
     nc = tc.nc
     with ExitStack() as ctx:
         keep = ctx.enter_context(tc.tile_pool(name="keep", bufs=1))
-        psum_h = ctx.enter_context(tc.psum_pool(name="psum_h", bufs=4))
-        psum_y = ctx.enter_context(tc.psum_pool(name="psum_y", bufs=4))
+        psum = ctx.enter_context(tc.psum_pool(name="psum", bufs=8))
 
         offsets = keep.tile([P, J // 16], U16, name="offsets")
         tab_s = keep.tile([P, T], U8, name="tab_s", align_bytes=64)
@@ -77,9 +76,9 @@ def tile_list_xcross_noneP_kernel(tc, tab_words, tab_scales, wb_words, wb_scales
 
         halves = range(J // HALF)
         lists = [offsets[:, h * HALF // 16 : (h + 1) * HALF // 16] for h in halves]
-        v_s = [keep.tile([P, HALF], U8, name="v_s%d" % h, align_bytes=64) for h in halves]
-        for h in halves:
-            nc.vector.tensor_copy(v_s[h][:], tab_s[:].indirect(lists[h]))
+        v_s_all = keep.tile([P, J], U8, name="v_s", align_bytes=64)
+        nc.vector.tensor_copy(v_s_all[:], tab_s[:].indirect(offsets[:]))
+        v_s = [v_s_all[:, h * HALF : (h + 1) * HALF] for h in halves]
         dn_w, dn_s = deal("dn", dn_w_raw, dn_s_raw)
         v_w = [
             keep.tile([P, HALF], U32, name="v_w0", align_bytes=64),
@@ -87,13 +86,22 @@ def tile_list_xcross_noneP_kernel(tc, tab_words, tab_scales, wb_words, wb_scales
         ]
         for h in halves:
             nc.vector.tensor_copy(v_w[h][:], tab_w[:].bitcast(U32).indirect(lists[h]))
-        wb_w, wb_s = deal("wb", wb_w_raw, wb_s_raw)
 
-        h_bf = [keep.tile([P, HALF, PACK], BF16, name="h_bf%d" % h, align_bytes=64) for h in halves]
+        up_bf = keep.tile([P, PACK * N], BF16, name="up_bf", align_bytes=64)
+        up_w = keep.tile([P, N], U32, name="up_w", align_bytes=64)
+        up_s = keep.tile([P, N], U8, name="up_s", align_bytes=64)
+        up_out = up_bf[:].rearrange("p (t m i) -> p m i t", t=PACK, i=PACK)
+        up_in = up_raw[:].rearrange("p i (m t) -> p m i t", t=PACK)
+        nc.vector.tensor_copy(up_out, up_in)
+        wb_w, wb_s = deal("wb", wb_w_raw, wb_s_raw)
+        nc.vector.quantize_mx(out=up_w[:].bitcast(FP8X4), scales=up_s[:], in_=up_bf[:])
+
+        h_all = keep.tile([P, J, PACK], BF16, name="h_bf", align_bytes=64)
+        h_bf = [h_all[:, h * HALF : (h + 1) * HALF, :] for h in halves]
         for h in halves:
             for c in range(HALF // HT):
                 cols = slice(c * HT, (c + 1) * HT)
-                bank = psum_h.tile([P, PACK, HT], F32, name="h_bank")
+                bank = psum.tile([P, PACK, HT], F32, name="h_bank", tag="bank")
                 for t in range(PACK):
                     nc.tensor.matmul_mx(
                         out=bank[:, t, :],
@@ -106,21 +114,12 @@ def tile_list_xcross_noneP_kernel(tc, tab_words, tab_scales, wb_words, wb_scales
                     )
                 nc.scalar.copy(h_bf[h][:, cols, :], bank[:].rearrange("p t j -> p j t"))
 
-        up_bf = keep.tile([P, PACK * N], BF16, name="up_bf", align_bytes=64)
-        up_w = keep.tile([P, N], U32, name="up_w", align_bytes=64)
-        up_s = keep.tile([P, N], U8, name="up_s", align_bytes=64)
-        nc.vector.tensor_copy(
-            up_bf[:].rearrange("p (t m i) -> p m i t", t=PACK, i=PACK),
-            up_raw[:].rearrange("p i (m t) -> p m i t", t=PACK),
-        )
-        nc.vector.quantize_mx(out=up_w[:].bitcast(FP8X4), scales=up_s[:], in_=up_bf[:])
-
         h_s = [keep.tile([P, HALF], U8, name="h_s%d" % h, align_bytes=64) for h in halves]
         h_w = {}
 
         def quantise_h(h, tag):
             h_w[h] = keep.tile([P, HALF], U32, name="h_w%d" % h, tag=tag, align_bytes=64)
-            nc.vector.quantize_mx(out=h_w[h][:].bitcast(FP8X4), scales=h_s[h][:], in_=h_bf[h][:].rearrange("p j t -> p (j t)"))
+            nc.vector.quantize_mx(out=h_w[h][:].bitcast(FP8X4), scales=h_s[h][:], in_=h_bf[h].rearrange("p j t -> p (j t)"))
 
         quantise_h(0, "h_w0")
 
@@ -130,25 +129,21 @@ def tile_list_xcross_noneP_kernel(tc, tab_words, tab_scales, wb_words, wb_scales
         out_words = out_1[0].rearrange("p j i -> p (j i)").bitcast(I32)
 
         def product(h, t):
-            bank = psum_y.tile([P, HALF], F32, name="y_bank")
-            nc.tensor.matmul_mx(
-                out=bank[:],
-                lhsT=wb_w[:, 2 * P * t : 2 * P * (t + 1)].bitcast(FP4X4),
-                lhsT_scale=wb_s[:, P * t : P * (t + 1)],
-                rhs=v_w[h][:].bitcast(FP8X4),
-                rhs_scale=v_s[h][:],
-                start=True,
-                stop=False,
-            )
-            nc.tensor.matmul_mx(
-                out=bank[:],
-                lhsT=up_w[:, P * t : P * (t + 1)].bitcast(FP8X4),
-                lhsT_scale=up_s[:, P * t : P * (t + 1)],
-                rhs=h_w[h][:].bitcast(FP8X4),
-                rhs_scale=h_s[h][:],
-                start=False,
-                stop=True,
-            )
+            bank = psum.tile([P, HALF], F32, name="y_bank", tag="bank")
+            cols = slice(P * t, P * (t + 1))
+            wb_pass = (wb_w[:, 2 * P * t : 2 * P * (t + 1)].bitcast(FP4X4), wb_s[:, cols], v_w[h][:], v_s[h])
+            up_pass = (up_w[:, cols].bitcast(FP8X4), up_s[:, cols], h_w[h][:], h_s[h][:])
+            passes = (wb_pass, up_pass) if h == 0 else (up_pass, wb_pass)
+            for n, (weight, weight_s, moving, moving_s) in enumerate(passes):
+                nc.tensor.matmul_mx(
+                    out=bank[:],
+                    lhsT=weight,
+                    lhsT_scale=weight_s,
+                    rhs=moving.bitcast(FP8X4),
+                    rhs_scale=moving_s,
+                    start=n == 0,
+                    stop=n == 1,
+                )
             return bank
 
         def biased(h, t, tag):
@@ -165,10 +160,8 @@ def tile_list_xcross_noneP_kernel(tc, tab_words, tab_scales, wb_words, wb_scales
         def store(res, j0, width, t0, t1):
             nc.sync.dma_start(out_rows[:, t0:t1, j0 : j0 + width], res[:, t0:t1, :])
 
-        def rounded(res, name, copy):
-            o_bf = keep.tile([P, res.shape[2], PACK], BF16, name=name, align_bytes=64)
-            copy(o_bf[:].rearrange("p (c i) t -> p c t i", i=4), res[:].rearrange("p t (c i) -> p c t i", i=4))
-            return o_bf
+        def round_and_weave(copy, o_bf, res):
+            copy(o_bf.rearrange("p (c i) t -> p c t i", i=4), res.rearrange("p t (c i) -> p c t i", i=4))
 
         def quantise(o_bf, j0, width):
             cols = slice(j0, j0 + width)
@@ -186,28 +179,30 @@ def tile_list_xcross_noneP_kernel(tc, tab_words, tab_scales, wb_words, wb_scales
         y_a = {t: biased(0, t, "y_a%d" % t) for t in range(1, PACK)}
         y_b = {t: biased(1, t, "y_b%d" % t) for t in range(PACK)}
 
-        cross(res_a, y_a[1], 0, HALF, 1)
-        store(res_a, 0, HALF, 1, 2)
-        res_b = keep.tile([P, PACK, QUART], F32, name="res_b", tag="y_a1", align_bytes=64)
-        for t in range(2, PACK):
-            cross(res_b, y_b[t - 2], HALF, QUART, t - 2)
+        for t in range(1, PACK):
             cross(res_a, y_a[t], 0, HALF, t)
             store(res_a, 0, HALF, t, t + 1)
-        store(res_b, HALF, QUART, 0, 2)
-        bf_a = rounded(res_a, "bf_a", nc.scalar.copy)
-        for t in range(2, PACK):
+        bf_first = keep.tile([P, QUART, PACK], BF16, name="bf_first", tag="bf_first", align_bytes=64)
+        bf_mid = keep.tile([P, HALF, PACK], BF16, name="bf_mid", align_bytes=64)
+        bf_last = keep.tile([P, QUART, PACK], BF16, name="bf_last", align_bytes=64)
+        round_and_weave(nc.scalar.copy, bf_first[:], res_a[:, :, :QUART])
+        round_and_weave(nc.scalar.copy, bf_mid[:, :QUART, :], res_a[:, :, QUART:])
+        res_b = keep.tile([P, PACK, QUART], F32, name="res_b", tag="y_a3", align_bytes=64)
+        for t in range(PACK):
             cross(res_b, y_b[t], HALF, QUART, t)
-        store(res_b, HALF, QUART, 2, 4)
-        bf_b = rounded(res_b, "bf_b", nc.scalar.copy)
-        res_c = keep.tile([P, PACK, QUART], F32, name="res_c", tag="y_a3", align_bytes=64)
+            if t % 2 == 1:
+                store(res_b, HALF, QUART, t - 1, t + 1)
+        round_and_weave(nc.scalar.copy, bf_mid[:, QUART:, :], res_b[:])
+        quantise(bf_first, 0, QUART)
+        res_c = keep.tile([P, PACK, QUART], F32, name="res_c", tag="bf_first", align_bytes=64)
         for t in range(PACK):
             cross(res_c, y_b[t], HALF + QUART, QUART, t)
             if t % 2 == 1:
                 store(res_c, HALF + QUART, QUART, t - 1, t + 1)
-        quantise(bf_a, 0, HALF)
-        bf_c = rounded(res_c, "bf_c", nc.vector.tensor_copy)
-        quantise(bf_b, HALF, QUART)
-        quantise(bf_c, HALF + QUART, QUART)
+        round_and_weave(nc.scalar.copy, bf_last[:, : QUART // 2, :], res_c[:, :, : QUART // 2])
+        round_and_weave(nc.vector.tensor_copy, bf_last[:, QUART // 2 :, :], res_c[:, :, QUART // 2 :])
+        quantise(bf_mid, QUART, HALF)
+        quantise(bf_last, HALF + QUART, QUART)
         for q in range(4):
             queue = nc.sync if q % 2 == 0 else nc.scalar
             queue.dma_start(out_2[0, 4 * q : 4 * q + 4, :].bitcast(I32), o_s[32 * q : 32 * q + 4, :].bitcast(I32))

@@ -25,7 +25,7 @@ HT = 128
 
 def load_scale_rows(queue, plane, scales):
     for q in range(4):
-        queue.dma_start(plane[32 * q : 32 * q + 32, :].bitcast(I32), scales[0, 4 * q : 4 * q + 4, :].bitcast(I32).partition_broadcast(8))
+        queue.dma_start(plane[32 * q : 32 * q + 4, :].bitcast(I32), scales[0, 4 * q : 4 * q + 4, :].bitcast(I32))
 
 
 def tile_list_xcross_noneP_kernel(tc, tab_words, tab_scales, wb_words, wb_scales, dn_words, dn_scales, upw, x0T, b, offs, out_0, out_1, out_2):
@@ -47,16 +47,20 @@ def tile_list_xcross_noneP_kernel(tc, tab_words, tab_scales, wb_words, wb_scales
         x0 = [keep.tile([P, T], F32, name="x0_%d" % t, align_bytes=64) for t in range(PACK)]
 
 
+        nc.gpsimd.memset(tab_s[:, : T // 2].bitcast(I32), 0)
+        for plane in (tab_s[:, T // 2 :], dn_s_raw[:], wb_s_raw[:]):
+            nc.vector.memset(plane.bitcast(I32), 0)
+
         x0_rows = x0T.rearrange("(p t) c -> p t c", t=PACK)
         nc.sync.dma_start(offsets[:], offs)
+        nc.sync.dma_start(dn_w_raw[:].bitcast(I32), dn_words[0].bitcast(I32))
+        nc.sync.dma_start(bias[:], b.rearrange("(p t) -> p t", t=PACK))
         load_scale_rows(nc.sync, tab_s, tab_scales)
         nc.sync.dma_start(tab_w[:], tab_words[0].rearrange("p t i -> p (t i)").bitcast(I32))
-        nc.sync.dma_start(dn_w_raw[:].bitcast(I32), dn_words[0].bitcast(I32))
         load_scale_rows(nc.sync, dn_s_raw, dn_scales)
         nc.sync.dma_start(up_raw[:], upw.rearrange("(p i) n -> p i n", i=PACK))
         nc.sync.dma_start(wb_w_raw[:].bitcast(I32), wb_words[0].bitcast(I32))
         load_scale_rows(nc.sync, wb_s_raw, wb_scales)
-        nc.sync.dma_start(bias[:], b.rearrange("(p t) -> p t", t=PACK))
         for t in range(PACK):
             nc.sync.dma_start(x0[t][:], x0_rows[:, t, :])
         nc.scalar.activation(bias1[:], bias[:], IDENT, bias=1.0)
@@ -179,30 +183,31 @@ def tile_list_xcross_noneP_kernel(tc, tab_words, tab_scales, wb_words, wb_scales
         y_a = {t: biased(0, t, "y_a%d" % t) for t in range(1, PACK)}
         y_b = {t: biased(1, t, "y_b%d" % t) for t in range(PACK)}
 
-        for t in range(1, PACK):
+        for t in (1, 2):
             cross(res_a, y_a[t], 0, HALF, t)
             store(res_a, 0, HALF, t, t + 1)
-        bf_first = keep.tile([P, QUART, PACK], BF16, name="bf_first", tag="bf_first", align_bytes=64)
-        bf_mid = keep.tile([P, HALF, PACK], BF16, name="bf_mid", align_bytes=64)
-        bf_last = keep.tile([P, QUART, PACK], BF16, name="bf_last", align_bytes=64)
-        round_and_weave(nc.scalar.copy, bf_first[:], res_a[:, :, :QUART])
-        round_and_weave(nc.scalar.copy, bf_mid[:, :QUART, :], res_a[:, :, QUART:])
-        res_b = keep.tile([P, PACK, QUART], F32, name="res_b", tag="y_a3", align_bytes=64)
-        for t in range(PACK):
+        res_b = keep.tile([P, PACK, QUART], F32, name="res_b", tag="y_a2", align_bytes=64)
+        for t in range(3):
             cross(res_b, y_b[t], HALF, QUART, t)
-            if t % 2 == 1:
-                store(res_b, HALF, QUART, t - 1, t + 1)
-        round_and_weave(nc.scalar.copy, bf_mid[:, QUART:, :], res_b[:])
-        quantise(bf_first, 0, QUART)
-        res_c = keep.tile([P, PACK, QUART], F32, name="res_c", tag="bf_first", align_bytes=64)
+        store(res_b, HALF, QUART, 0, 2)
+        cross(res_a, y_a[3], 0, HALF, 3)
+        store(res_a, 0, HALF, 3, 4)
+        bf_a = keep.tile([P, HALF, PACK], BF16, name="bf_a", tag="bf_a", align_bytes=64)
+        bf_b = keep.tile([P, QUART, PACK], BF16, name="bf_b", align_bytes=64)
+        round_and_weave(nc.scalar.copy, bf_a[:], res_a[:])
+        cross(res_b, y_b[3], HALF, QUART, 3)
+        store(res_b, HALF, QUART, 2, 4)
+        round_and_weave(nc.scalar.copy, bf_b[:], res_b[:])
+        res_c = keep.tile([P, PACK, QUART], F32, name="res_c", tag="y_a3", align_bytes=64)
         for t in range(PACK):
             cross(res_c, y_b[t], HALF + QUART, QUART, t)
             if t % 2 == 1:
                 store(res_c, HALF + QUART, QUART, t - 1, t + 1)
-        round_and_weave(nc.scalar.copy, bf_last[:, : QUART // 2, :], res_c[:, :, : QUART // 2])
-        round_and_weave(nc.vector.tensor_copy, bf_last[:, QUART // 2 :, :], res_c[:, :, QUART // 2 :])
-        quantise(bf_mid, QUART, HALF)
-        quantise(bf_last, HALF + QUART, QUART)
+        quantise(bf_a, 0, HALF)
+        bf_c = keep.tile([P, QUART, PACK], BF16, name="bf_c", tag="bf_a", align_bytes=64)
+        round_and_weave(nc.vector.tensor_copy, bf_c[:], res_c[:])
+        quantise(bf_b, HALF, QUART)
+        quantise(bf_c, HALF + QUART, QUART)
         for q in range(4):
             queue = nc.sync if q % 2 == 0 else nc.scalar
             queue.dma_start(out_2[0, 4 * q : 4 * q + 4, :].bitcast(I32), o_s[32 * q : 32 * q + 4, :].bitcast(I32))

@@ -14,17 +14,16 @@ U8 = mybir.dt.uint8
 FP8X4 = mybir.dt.float8_e4m3fn_x4
 FP4X4 = mybir.dt.float4_e2m1fn_x4
 MULT = mybir.AluOpType.mult
-ADD = mybir.AluOpType.add
 IDENT = mybir.ActivationFunctionType.Identity
 
 P = 128
 PACK = 4
-HALF = 512
-HT = 128
+PASS_N = 128
+CHUNK = 256
 
 
-def load_scale_rows(queue, plane, scales):
-    for q in range(4):
+def load_scale_rows(queue, plane, scales, quadrants=range(4)):
+    for q in quadrants:
         queue.dma_start(plane[32 * q : 32 * q + 4, :].bitcast(I32), scales[0, 4 * q : 4 * q + 4, :].bitcast(I32))
 
 
@@ -34,180 +33,232 @@ def tile_list_xcross_noneP_kernel(tc, tab_words, tab_scales, wb_words, wb_scales
         keep = ctx.enter_context(tc.tile_pool(name="keep", bufs=1))
         psum = ctx.enter_context(tc.psum_pool(name="psum", bufs=8))
 
-        offsets = keep.tile([P, J // 16], U16, name="offsets")
-        tab_s = keep.tile([P, T], U8, name="tab_s", align_bytes=64)
-        tab_w = keep.tile([P, T], I32, name="tab_w", align_bytes=64)
-        dn_s_raw = keep.tile([P, R], U8, name="dn_s_raw", tag="reused", align_bytes=64)
-        wb_s_raw = keep.tile([P, N], U8, name="wb_s_raw", align_bytes=64)
-        dn_w_raw = keep.tile([P, 2 * R], U8, name="dn_w_raw", align_bytes=64)
-        wb_w_raw = keep.tile([P, 2 * N], U8, name="wb_w_raw", align_bytes=64)
-        up_raw = keep.tile([P, PACK, N], F32, name="up_raw", align_bytes=64)
-        bias = keep.tile([P, PACK], F32, name="bias")
-        bias1 = keep.tile([P, PACK], F32, name="bias1")
-        x0 = [keep.tile([P, T], F32, name="x0_%d" % t, align_bytes=64) for t in range(PACK)]
+        shared = ctx.enter_context(tc.tile_pool(name="shared", bufs=1))
 
+        def sbuf(name, shape, dtype, tag=None):
+            if isinstance(tag, int):
+                return shared.tile(shape, dtype, name=name, align_bytes=64, offset=tag)
+            return keep.tile(shape, dtype, name=name, tag=tag or name, align_bytes=64)
+
+        offsets = keep.tile([P, J // 16], U16, name="offsets")
+        tab_s = sbuf("tab_s", [P, T], U8)
+        tab_w = sbuf("tab_w", [P, T], I32)
+        dn_s_raw = sbuf("dn_s_raw", [P, R], U8, 5888)
+        wb_s_raw = sbuf("wb_s_raw", [P, N], U8, 4096)
+        dn_w_raw = sbuf("dn_w_raw", [P, 2 * R], U8)
+        wb_w_raw = sbuf("wb_w_raw", [P, 2 * N], U8)
+        up_raw = [sbuf("up_raw0", [P, PACK, N // 2], F32, 0), sbuf("up_raw1", [P, PACK, N // 2], F32)]
+        bias = sbuf("bias", [P, PACK], F32)
+        bias1 = sbuf("bias1", [P, PACK], F32)
+        x0 = [sbuf("x0_%d" % t, [P, T], F32) for t in range(PACK)]
 
         nc.gpsimd.memset(tab_s[:, : T // 2].bitcast(I32), 0)
         for plane in (tab_s[:, T // 2 :], dn_s_raw[:], wb_s_raw[:]):
             nc.vector.memset(plane.bitcast(I32), 0)
 
         x0_rows = x0T.rearrange("(p t) c -> p t c", t=PACK)
+        up_rows = upw.rearrange("(p i) n -> p i n", i=PACK)
         nc.sync.dma_start(offsets[:], offs)
         nc.sync.dma_start(dn_w_raw[:].bitcast(I32), dn_words[0].bitcast(I32))
-        nc.sync.dma_start(bias[:], b.rearrange("(p t) -> p t", t=PACK))
+        nc.sync.dma_start(wb_w_raw[:].bitcast(I32), wb_words[0].bitcast(I32))
         load_scale_rows(nc.sync, tab_s, tab_scales)
         nc.sync.dma_start(tab_w[:], tab_words[0].rearrange("p t i -> p (t i)").bitcast(I32))
         load_scale_rows(nc.sync, dn_s_raw, dn_scales)
-        nc.sync.dma_start(up_raw[:], upw.rearrange("(p i) n -> p i n", i=PACK))
-        nc.sync.dma_start(wb_w_raw[:].bitcast(I32), wb_words[0].bitcast(I32))
-        load_scale_rows(nc.sync, wb_s_raw, wb_scales)
-        for t in range(PACK):
+        for u in range(2):
+            nc.sync.dma_start(up_raw[u][:], up_rows[:, :, u * N // 2 : (u + 1) * N // 2])
+        load_scale_rows(nc.gpsimd, wb_s_raw, wb_scales, range(3))
+        load_scale_rows(nc.sync, wb_s_raw, wb_scales, range(3, 4))
+        nc.sync.dma_start(x0[0][:], x0_rows[:, 0, :])
+        nc.sync.dma_start(bias[:], b.rearrange("(p t) -> p t", t=PACK))
+        for t in range(1, PACK):
             nc.sync.dma_start(x0[t][:], x0_rows[:, t, :])
-        nc.scalar.activation(bias1[:], bias[:], IDENT, bias=1.0)
 
-        def deal(name, words_raw, scales_raw):
-            words = keep.tile([P, 2 * N], U8, name=name + "_w", align_bytes=64)
-            scales = keep.tile([P, N], U8, name=name + "_s", align_bytes=64)
+        def deal_words(name, raw):
+            words = sbuf(name, [P, 2 * N], U8)
             nc.vector.tensor_copy(
                 words[:].bitcast(U16).rearrange("p (t m) -> p t m", t=PACK),
-                words_raw[:].bitcast(U16).rearrange("p (m t) -> p t m", t=PACK),
+                raw[:].bitcast(U16).rearrange("p (m t) -> p t m", t=PACK),
             )
+            return words
+
+        def deal_scales(name, raw, tag=None):
+            scales = sbuf(name, [P, N], U8, tag)
             nc.vector.tensor_copy(
                 scales[:].rearrange("p (t m) -> p t m", t=PACK),
-                scales_raw[:].rearrange("p (m t) -> p t m", t=PACK),
+                raw[:].rearrange("p (m t) -> p t m", t=PACK),
             )
-            return words, scales
+            return scales
 
-        halves = range(J // HALF)
-        lists = [offsets[:, h * HALF // 16 : (h + 1) * HALF // 16] for h in halves]
-        v_s_all = keep.tile([P, J], U8, name="v_s", align_bytes=64)
-        nc.vector.tensor_copy(v_s_all[:], tab_s[:].indirect(offsets[:]))
-        v_s = [v_s_all[:, h * HALF : (h + 1) * HALF] for h in halves]
-        dn_w, dn_s = deal("dn", dn_w_raw, dn_s_raw)
-        v_w = [
-            keep.tile([P, HALF], U32, name="v_w0", align_bytes=64),
-            keep.tile([P, HALF], U32, name="v_w1", tag="reused", align_bytes=64),
-        ]
-        for h in halves:
-            nc.vector.tensor_copy(v_w[h][:], tab_w[:].bitcast(U32).indirect(lists[h]))
+        def entries(c):
+            return offsets[:, c * CHUNK // 16 : (c + 1) * CHUNK // 16]
 
-        up_bf = keep.tile([P, PACK * N], BF16, name="up_bf", align_bytes=64)
-        up_w = keep.tile([P, N], U32, name="up_w", align_bytes=64)
-        up_s = keep.tile([P, N], U8, name="up_s", align_bytes=64)
-        up_out = up_bf[:].rearrange("p (t m i) -> p m i t", t=PACK, i=PACK)
-        up_in = up_raw[:].rearrange("p i (m t) -> p m i t", t=PACK)
-        nc.vector.tensor_copy(up_out, up_in)
-        wb_w, wb_s = deal("wb", wb_w_raw, wb_s_raw)
-        nc.vector.quantize_mx(out=up_w[:].bitcast(FP8X4), scales=up_s[:], in_=up_bf[:])
+        def span(c):
+            return slice(c * CHUNK, (c + 1) * CHUNK)
 
-        h_all = keep.tile([P, J, PACK], BF16, name="h_bf", align_bytes=64)
-        h_bf = [h_all[:, h * HALF : (h + 1) * HALF, :] for h in halves]
-        for h in halves:
-            for c in range(HALF // HT):
-                cols = slice(c * HT, (c + 1) * HT)
-                bank = psum.tile([P, PACK, HT], F32, name="h_bank", tag="bank")
-                for t in range(PACK):
-                    nc.tensor.matmul_mx(
-                        out=bank[:, t, :],
-                        lhsT=dn_w[:, 2 * P * t : 2 * P * (t + 1)].bitcast(FP4X4),
-                        lhsT_scale=dn_s[:, P * t : P * (t + 1)],
-                        rhs=v_w[h][:, cols].bitcast(FP8X4),
-                        rhs_scale=v_s[h][:, cols],
-                        start=True,
-                        stop=True,
-                    )
-                nc.scalar.copy(h_bf[h][:, cols, :], bank[:].rearrange("p t j -> p j t"))
-
-        h_s = [keep.tile([P, HALF], U8, name="h_s%d" % h, align_bytes=64) for h in halves]
-        h_w = {}
-
-        def quantise_h(h, tag):
-            h_w[h] = keep.tile([P, HALF], U32, name="h_w%d" % h, tag=tag, align_bytes=64)
-            nc.vector.quantize_mx(out=h_w[h][:].bitcast(FP8X4), scales=h_s[h][:], in_=h_bf[h].rearrange("p j t -> p (j t)"))
-
-        quantise_h(0, "h_w0")
-
-        o_w = keep.tile([P, J], I32, name="o_w", align_bytes=64)
-        o_s = keep.tile([P, J], U8, name="o_s", align_bytes=64)
+        A, B, C, D = range(J // CHUNK)
+        v_s = sbuf("v_s", [P, J], U8)
+        up_bf = sbuf("up_bf", [P, PACK * N], BF16)
+        up_w = sbuf("up_w", [P, N], U32)
+        up_s = sbuf("up_s", [P, N], U8, 4352)
+        h_s = [sbuf("h_s%d" % c, [P, CHUNK], U8, 4096 if c == A else None) for c in (A, B, C, D)]
+        o_w = sbuf("o_w", [P, J], I32)
+        o_s = sbuf("o_s", [P, J], U8)
+        res = [sbuf("res%d" % c, [P, PACK, CHUNK], F32) for c in (A, B, C, D)]
         out_rows = out_0.rearrange("(p t) j -> p t j", t=PACK)
         out_words = out_1[0].rearrange("p j i -> p (j i)").bitcast(I32)
+        v_w, h_bf, h_w, y1 = {}, {}, {}, {}
 
-        def product(h, t):
-            bank = psum.tile([P, HALF], F32, name="y_bank", tag="bank")
-            cols = slice(P * t, P * (t + 1))
-            wb_pass = (wb_w[:, 2 * P * t : 2 * P * (t + 1)].bitcast(FP4X4), wb_s[:, cols], v_w[h][:], v_s[h])
-            up_pass = (up_w[:, cols].bitcast(FP8X4), up_s[:, cols], h_w[h][:], h_s[h][:])
-            passes = (wb_pass, up_pass) if h == 0 else (up_pass, wb_pass)
-            for n, (weight, weight_s, moving, moving_s) in enumerate(passes):
+        def new_bank(held):
+            return psum.tile([P, 2 * CHUNK], F32, name="bank", tag=held or "ring", bufs=1 if held else 6)[:]
+
+        def round_up(copy, u):
+            copy(
+                up_bf[:].rearrange("p (t u m i) -> p u m i t", t=PACK, u=2, i=PACK)[:, u],
+                up_raw[u][:].rearrange("p i (m t) -> p m i t", t=PACK),
+            )
+
+        def gather_words(c, tag=None):
+            v_w[c] = sbuf("v_w%d" % c, [P, CHUNK], U32, tag)
+            nc.vector.tensor_copy(v_w[c][:], tab_w[:].bitcast(U32).indirect(entries(c)))
+
+        def first_product(c, piece, held=None):
+            if piece == 0:
+                h_bf[c] = sbuf("h_bf%d" % c, [P, CHUNK, PACK], BF16, 2048 * c if c in (A, B) else None)
+            cols = slice(piece * PASS_N, (piece + 1) * PASS_N)
+            bank = new_bank(held).rearrange("p (t j) -> p t j", t=PACK)
+            for t in range(PACK):
                 nc.tensor.matmul_mx(
-                    out=bank[:],
-                    lhsT=weight,
-                    lhsT_scale=weight_s,
-                    rhs=moving.bitcast(FP8X4),
-                    rhs_scale=moving_s,
-                    start=n == 0,
-                    stop=n == 1,
+                    out=bank[:, t, :],
+                    lhsT=dn_w[:, 2 * P * t : 2 * P * (t + 1)].bitcast(FP4X4),
+                    lhsT_scale=dn_s[:, P * t : P * (t + 1)],
+                    rhs=v_w[c][:, cols].bitcast(FP8X4),
+                    rhs_scale=v_s[:, span(c)][:, cols],
+                    start=True,
+                    stop=True,
                 )
-            return bank
+            nc.scalar.copy(h_bf[c][:, cols, :], bank.rearrange("p t j -> p j t"))
 
-        def biased(h, t, tag):
-            bank = product(h, t)
-            y1 = keep.tile([P, HALF], F32, name="y1_%d_%d" % (h, t), tag=tag, align_bytes=64)
-            nc.scalar.activation(y1[:], bank[:], IDENT, bias=bias1[:, t : t + 1])
-            return y1
+        def quantise_h(c, tag=None):
+            h_w[c] = sbuf("h_w%d" % c, [P, CHUNK], U32, tag)
+            nc.vector.quantize_mx(out=h_w[c][:].bitcast(FP8X4), scales=h_s[c][:], in_=h_bf[c][:].rearrange("p j t -> p (j t)"))
 
-        def cross(res, y1, j0, width, t):
-            part = offsets[:, j0 // 16 : (j0 + width) // 16]
-            c0 = j0 % HALF
-            nc.vector.tensor_tensor(res[:, t, :], x0[t][:].indirect(part), y1[:, c0 : c0 + width], MULT)
+        def second_product(chunks, t, dest=None, held=None):
+            width = CHUNK * len(chunks)
+            bank = new_bank(held)
+            rows = slice(P * t, P * (t + 1))
+            for n, c in enumerate(chunks):
+                for piece in range(CHUNK // PASS_N):
+                    cols = slice(piece * PASS_N, (piece + 1) * PASS_N)
+                    sums = bank[:, n * CHUNK : (n + 1) * CHUNK][:, cols]
+                    nc.tensor.matmul_mx(
+                        out=sums,
+                        lhsT=up_w[:, rows].bitcast(FP8X4),
+                        lhsT_scale=up_s[:, rows],
+                        rhs=h_w[c][:, cols].bitcast(FP8X4),
+                        rhs_scale=h_s[c][:, cols],
+                        start=True,
+                        stop=False,
+                    )
+                    nc.tensor.matmul_mx(
+                        out=sums,
+                        lhsT=wb_w[:, 2 * P * t : 2 * P * (t + 1)].bitcast(FP4X4),
+                        lhsT_scale=wb_s[:, rows],
+                        rhs=v_w[c][:, cols].bitcast(FP8X4),
+                        rhs_scale=v_s[:, span(c)][:, cols],
+                        start=False,
+                        stop=True,
+                    )
+            if dest is None:
+                dest = sbuf("y1_%d_%d" % (chunks[0], t), [P, width], F32)[:]
+            nc.scalar.activation(dest, bank[:, :width], IDENT, bias=bias1[:, t : t + 1])
+            for n, c in enumerate(chunks):
+                y1[c, t] = dest[:, n * CHUNK : (n + 1) * CHUNK]
 
-        def store(res, j0, width, t0, t1):
-            nc.sync.dma_start(out_rows[:, t0:t1, j0 : j0 + width], res[:, t0:t1, :])
+        def cross(c, t, part=slice(0, CHUNK)):
+            picks = entries(c)[:, part.start // 16 : part.stop // 16]
+            nc.vector.tensor_tensor(res[c][:, t, part], x0[t][:].indirect(picks), y1[c, t][:, part], MULT)
 
-        def round_and_weave(copy, o_bf, res):
-            copy(o_bf.rearrange("p (c i) t -> p c t i", i=4), res.rearrange("p t (c i) -> p c t i", i=4))
+        def store(c, t0, t1):
+            nc.sync.dma_start(out_rows[:, t0:t1, span(c)], res[c][:, t0:t1, :])
 
-        def quantise(o_bf, j0, width):
-            cols = slice(j0, j0 + width)
-            nc.vector.quantize_mx(out=o_w[:, cols].bitcast(FP8X4), scales=o_s[:, cols], in_=o_bf[:].rearrange("p j t -> p (j t)"))
+        def weave(c, dest, part=slice(0, CHUNK)):
+            nc.scalar.copy(dest[:, part, :].rearrange("p (c i) t -> p c t i", i=4), res[c][:, :, part].rearrange("p t (c i) -> p c t i", i=4))
+
+        def quantise_out(src, cols):
+            nc.vector.quantize_mx(out=o_w[:, cols].bitcast(FP8X4), scales=o_s[:, cols], in_=src.rearrange("p j t -> p (j t)"))
             nc.sync.dma_start(out_words[:, cols], o_w[:, cols])
 
-        QUART = HALF // 2
-        res_a = keep.tile([P, PACK, HALF], F32, name="res_a", align_bytes=64)
-        bank = product(0, 0)
-        picked = keep.tile([P, HALF], F32, name="picked", tag="picked", align_bytes=64)
-        nc.vector.tensor_copy(picked[:], x0[0][:].indirect(lists[0]))
-        nc.vector.scalar_tensor_tensor(res_a[:, 0, :], bank[:], bias1[:, 0:1], picked[:], ADD, MULT)
-        store(res_a, 0, HALF, 0, 1)
-        quantise_h(1, "picked")
-        y_a = {t: biased(0, t, "y_a%d" % t) for t in range(1, PACK)}
-        y_b = {t: biased(1, t, "y_b%d" % t) for t in range(PACK)}
+        def flat(c):
+            return res[c][:].rearrange("p t j -> p (t j)")
 
-        for t in (1, 2):
-            cross(res_a, y_a[t], 0, HALF, t)
-            store(res_a, 0, HALF, t, t + 1)
-        res_b = keep.tile([P, PACK, QUART], F32, name="res_b", tag="y_a2", align_bytes=64)
-        for t in range(3):
-            cross(res_b, y_b[t], HALF, QUART, t)
-        store(res_b, HALF, QUART, 0, 2)
-        cross(res_a, y_a[3], 0, HALF, 3)
-        store(res_a, 0, HALF, 3, 4)
-        bf_a = keep.tile([P, HALF, PACK], BF16, name="bf_a", tag="bf_a", align_bytes=64)
-        bf_b = keep.tile([P, QUART, PACK], BF16, name="bf_b", align_bytes=64)
-        round_and_weave(nc.scalar.copy, bf_a[:], res_a[:])
-        cross(res_b, y_b[3], HALF, QUART, 3)
-        store(res_b, HALF, QUART, 2, 4)
-        round_and_weave(nc.scalar.copy, bf_b[:], res_b[:])
-        res_c = keep.tile([P, PACK, QUART], F32, name="res_c", tag="y_a3", align_bytes=64)
+        dn_w = deal_words("dn_w", dn_w_raw)
+        wb_w = deal_words("wb_w", wb_w_raw)
+        nc.vector.tensor_copy(v_s[:], tab_s[:].indirect(offsets[:]))
+        gather_words(A)
+        dn_s = deal_scales("dn_s", dn_s_raw)
+        gather_words(B, 5120)
+        gather_words(C, 6144)
+        round_up(nc.scalar.copy, 0)
+        first_product(A, 0)
+        first_product(A, 1)
+        first_product(B, 0, held="held1")
+        first_product(B, 1, held="held2")
+        round_up(nc.vector.tensor_copy, 1)
+        wb_s = deal_scales("wb_s", wb_s_raw)
+        nc.vector.quantize_mx(out=up_w[:].bitcast(FP8X4), scales=up_s[:], in_=up_bf[:])
+        quantise_h(A)
+        gather_words(D, 0)
+        quantise_h(B)
+        first_product(C, 0, held="held1")
+        first_product(C, 1, held="held2")
+        quantise_h(C)
+        nc.scalar.activation(bias1[:], bias[:], IDENT, bias=1.0)
+        second_product([A], 0)
+        second_product([B], 0)
+        cross(A, 0)
+        cross(B, 0)
+        second_product([A, B], 1, flat(C)[:, : 2 * CHUNK])
+        second_product([C], 0, res[B][:, 2, :], held="held1")
+        second_product([C], 1, res[A][:, 2, :], held="held2")
+        first_product(D, 0, held="held1")
+        second_product([A, B], 2)
+        first_product(D, 1, held="held2")
+        for c in (A, B):
+            cross(c, 1)
+            store(c, 0, 2)
+        cross(C, 0)
+        cross(C, 1)
+        store(C, 0, 2)
+        quantise_h(D)
+        second_product([C], 2)
+        second_product([A, B], 3, flat(D)[:, CHUNK // 2 : 5 * CHUNK // 2])
+        second_product([C], 3)
         for t in range(PACK):
-            cross(res_c, y_b[t], HALF + QUART, QUART, t)
-            if t % 2 == 1:
-                store(res_c, HALF + QUART, QUART, t - 1, t + 1)
-        quantise(bf_a, 0, HALF)
-        bf_c = keep.tile([P, QUART, PACK], BF16, name="bf_c", tag="bf_a", align_bytes=64)
-        round_and_weave(nc.vector.tensor_copy, bf_c[:], res_c[:])
-        quantise(bf_b, HALF, QUART)
-        quantise(bf_c, HALF + QUART, QUART)
+            second_product([D], t)
+        for c in (A, B, C):
+            cross(c, 2)
+            store(c, 2, 3)
+        bf_ab = sbuf("bf_ab", [P, 2 * CHUNK, PACK], BF16)
+        bf_c = sbuf("bf_c", [P, CHUNK, PACK], BF16)
+        bf_d = sbuf("bf_d", [P, CHUNK, PACK], BF16)
+        for c, dest in ((A, bf_ab[:, span(A), :]), (B, bf_ab[:, span(B), :]), (C, bf_c[:])):
+            cross(c, 3)
+            store(c, 3, 4)
+            weave(c, dest)
+        cross(D, 0)
+        cross(D, 1)
+        store(D, 0, 2)
+        cross(D, 2)
+        store(D, 2, 3)
+        halves = [slice(0, CHUNK // 2), slice(CHUNK // 2, CHUNK)]
+        for part in halves:
+            cross(D, 3, part)
+        store(D, 3, 4)
+        for part in halves:
+            weave(D, bf_d[:], part)
+        quantise_out(bf_ab[:], slice(0, 2 * CHUNK))
+        quantise_out(bf_c[:], span(C))
+        quantise_out(bf_d[:], span(D))
         for q in range(4):
             queue = nc.sync if q % 2 == 0 else nc.scalar
             queue.dma_start(out_2[0, 4 * q : 4 * q + 4, :].bitcast(I32), o_s[32 * q : 32 * q + 4, :].bitcast(I32))

@@ -14,6 +14,7 @@ U8 = mybir.dt.uint8
 FP8X4 = mybir.dt.float8_e4m3fn_x4
 FP4X4 = mybir.dt.float4_e2m1fn_x4
 MULT = mybir.AluOpType.mult
+ADD = mybir.AluOpType.add
 IDENT = mybir.ActivationFunctionType.Identity
 
 P = 128
@@ -22,9 +23,9 @@ PASS_N = 128
 CHUNK = 256
 
 
-def load_scale_rows(queue, plane, scales, quadrants=range(4)):
-    for q in quadrants:
-        queue.dma_start(plane[32 * q : 32 * q + 4, :].bitcast(I32), scales[0, 4 * q : 4 * q + 4, :].bitcast(I32))
+def load_scale_rows(queue, plane, scales):
+    for r in range(4):
+        queue.dma_start(plane[r:P:32, :].bitcast(I32), scales[0, r:16:4, :].bitcast(I32))
 
 
 def tile_list_xcross_noneP_kernel(tc, tab_words, tab_scales, wb_words, wb_scales, dn_words, dn_scales, upw, x0T, b, offs, out_0, out_1, out_2):
@@ -58,19 +59,17 @@ def tile_list_xcross_noneP_kernel(tc, tab_words, tab_scales, wb_words, wb_scales
 
         x0_rows = x0T.rearrange("(p t) c -> p t c", t=PACK)
         up_rows = upw.rearrange("(p i) n -> p i n", i=PACK)
-        nc.sync.dma_start(offsets[:], offs)
         nc.sync.dma_start(dn_w_raw[:].bitcast(I32), dn_words[0].bitcast(I32))
         nc.sync.dma_start(wb_w_raw[:].bitcast(I32), wb_words[0].bitcast(I32))
+        nc.sync.dma_start(offsets[:], offs)
         load_scale_rows(nc.sync, tab_s, tab_scales)
         nc.sync.dma_start(tab_w[:], tab_words[0].rearrange("p t i -> p (t i)").bitcast(I32))
         load_scale_rows(nc.sync, dn_s_raw, dn_scales)
         for u in range(2):
             nc.sync.dma_start(up_raw[u][:], up_rows[:, :, u * N // 2 : (u + 1) * N // 2])
-        load_scale_rows(nc.gpsimd, wb_s_raw, wb_scales, range(3))
-        load_scale_rows(nc.sync, wb_s_raw, wb_scales, range(3, 4))
-        nc.sync.dma_start(x0[0][:], x0_rows[:, 0, :])
+        load_scale_rows(nc.sync, wb_s_raw, wb_scales)
         nc.sync.dma_start(bias[:], b.rearrange("(p t) -> p t", t=PACK))
-        for t in range(1, PACK):
+        for t in range(PACK):
             nc.sync.dma_start(x0[t][:], x0_rows[:, t, :])
 
         def deal_words(name, raw):
@@ -259,6 +258,6 @@ def tile_list_xcross_noneP_kernel(tc, tab_words, tab_scales, wb_words, wb_scales
         quantise_out(bf_ab[:], slice(0, 2 * CHUNK))
         quantise_out(bf_c[:], span(C))
         quantise_out(bf_d[:], span(D))
-        for q in range(4):
-            queue = nc.sync if q % 2 == 0 else nc.scalar
-            queue.dma_start(out_2[0, 4 * q : 4 * q + 4, :].bitcast(I32), o_s[32 * q : 32 * q + 4, :].bitcast(I32))
+        for r in range(4):
+            queue = nc.sync if r % 2 == 0 else nc.scalar
+            queue.dma_start(out_2[0, r:16:4, :].bitcast(I32), o_s[r:P:32, :].bitcast(I32))

@@ -229,21 +229,20 @@ def tile_list_xcross_noneP_kernel(tc, tab_words, tab_scales, wb_words, wb_scales
         cross(C, 1)
         store(C, 0, 2)
         quantise_h(D)
-        second_product([C], 2)
-        second_product([A, B], 3, flat(D)[:, CHUNK // 2 : 5 * CHUNK // 2])
-        second_product([C], 3)
+        second_product([A, B], 3, flat(C)[:, 2 * CHUNK :])
+        second_product([C], 2, flat(D)[:, CHUNK // 2 : 3 * CHUNK // 2])
+        second_product([C], 3, res[D][:, 2, :])
         for t in range(PACK):
             second_product([D], t)
-        for c in (A, B, C):
-            cross(c, 2)
-            store(c, 2, 3)
         bf_ab = sbuf("bf_ab", [P, 2 * CHUNK, PACK], BF16)
         bf_c = sbuf("bf_c", [P, CHUNK, PACK], BF16)
         bf_d = sbuf("bf_d", [P, CHUNK, PACK], BF16)
-        for c, dest in ((A, bf_ab[:, span(A), :]), (B, bf_ab[:, span(B), :]), (C, bf_c[:])):
-            cross(c, 3)
-            store(c, 3, 4)
-            weave(c, dest)
+        woven = {A: bf_ab[:, span(A), :], B: bf_ab[:, span(B), :], C: bf_c[:]}
+        for c, t in ((A, 2), (B, 2), (A, 3), (B, 3), (C, 2), (C, 3)):
+            cross(c, t)
+            store(c, t, t + 1)
+            if t == PACK - 1:
+                weave(c, woven[c])
         cross(D, 0)
         cross(D, 1)
         store(D, 0, 2)

@@ -21,6 +21,7 @@ P = 128
 PACK = 4
 PASS_N = 128
 CHUNK = 256
+UP_SPLIT = 192
 
 
 def load_scale_rows(queue, plane, scales):
@@ -48,7 +49,8 @@ def tile_list_xcross_noneP_kernel(tc, tab_words, tab_scales, wb_words, wb_scales
         wb_s_raw = sbuf("wb_s_raw", [P, N], U8, 4096)
         dn_w_raw = sbuf("dn_w_raw", [P, 2 * R], U8)
         wb_w_raw = sbuf("wb_w_raw", [P, 2 * N], U8)
-        up_raw = [sbuf("up_raw0", [P, PACK, N // 2], F32, 0), sbuf("up_raw1", [P, PACK, N // 2], F32)]
+        up_cols = [slice(0, UP_SPLIT), slice(UP_SPLIT, N)]
+        up_raw = [sbuf("up_raw0", [P, PACK, UP_SPLIT], F32, 0), sbuf("up_raw1", [P, PACK, N - UP_SPLIT], F32)]
         bias = sbuf("bias", [P, PACK], F32)
         bias1 = sbuf("bias1", [P, PACK], F32)
         x0 = [sbuf("x0_%d" % t, [P, T], F32) for t in range(PACK)]
@@ -66,7 +68,7 @@ def tile_list_xcross_noneP_kernel(tc, tab_words, tab_scales, wb_words, wb_scales
         nc.sync.dma_start(tab_w[:], tab_words[0].rearrange("p t i -> p (t i)").bitcast(I32))
         load_scale_rows(nc.sync, dn_s_raw, dn_scales)
         for u in range(2):
-            nc.sync.dma_start(up_raw[u][:], up_rows[:, :, u * N // 2 : (u + 1) * N // 2])
+            nc.sync.dma_start(up_raw[u][:], up_rows[:, :, up_cols[u]])
         load_scale_rows(nc.sync, wb_s_raw, wb_scales)
         nc.sync.dma_start(bias[:], b.rearrange("(p t) -> p t", t=PACK))
         for t in range(PACK):
@@ -102,7 +104,10 @@ def tile_list_xcross_noneP_kernel(tc, tab_words, tab_scales, wb_words, wb_scales
         h_s = [sbuf("h_s%d" % c, [P, CHUNK], U8, 4096 if c == A else None) for c in (A, B, C, D)]
         o_w = sbuf("o_w", [P, J], I32)
         o_s = sbuf("o_s", [P, J], U8)
-        res = [sbuf("res%d" % c, [P, PACK, CHUNK], F32) for c in (A, B, C, D)]
+        res_ab = sbuf("res_ab", [P, PACK, 2 * CHUNK], F32)
+        res_c = sbuf("res_c", [P, PACK, CHUNK], F32)
+        res_d = sbuf("res_d", [P, PACK, CHUNK], F32)
+        res = [res_ab[:, :, span(A)], res_ab[:, :, span(B)], res_c[:], res_d[:]]
         out_rows = out_0.rearrange("(p t) j -> p t j", t=PACK)
         out_words = out_1[0].rearrange("p j i -> p (j i)").bitcast(I32)
         v_w, h_bf, h_w, y1 = {}, {}, {}, {}
@@ -112,7 +117,7 @@ def tile_list_xcross_noneP_kernel(tc, tab_words, tab_scales, wb_words, wb_scales
 
         def round_up(copy, u):
             copy(
-                up_bf[:].rearrange("p (t u m i) -> p u m i t", t=PACK, u=2, i=PACK)[:, u],
+                up_bf[:].rearrange("p (t m i) -> p m i t", t=PACK, i=PACK)[:, up_cols[u].start // PACK : up_cols[u].stop // PACK],
                 up_raw[u][:].rearrange("p i (m t) -> p m i t", t=PACK),
             )
 
@@ -180,6 +185,9 @@ def tile_list_xcross_noneP_kernel(tc, tab_words, tab_scales, wb_words, wb_scales
         def store(c, t0, t1):
             nc.sync.dma_start(out_rows[:, t0:t1, span(c)], res[c][:, t0:t1, :])
 
+        def store_ab(t0, t1):
+            nc.sync.dma_start(out_rows[:, t0:t1, : 2 * CHUNK], res_ab[:, t0:t1, :])
+
         def weave(c, dest, part=slice(0, CHUNK)):
             nc.scalar.copy(dest[:, part, :].rearrange("p (c i) t -> p c t i", i=4), res[c][:, :, part].rearrange("p t (c i) -> p c t i", i=4))
 
@@ -188,7 +196,7 @@ def tile_list_xcross_noneP_kernel(tc, tab_words, tab_scales, wb_words, wb_scales
             nc.sync.dma_start(out_words[:, cols], o_w[:, cols])
 
         def flat(c):
-            return res[c][:].rearrange("p t j -> p (t j)")
+            return res[c].rearrange("p t j -> p (t j)")
 
         dn_w = deal_words("dn_w", dn_w_raw)
         wb_w = deal_words("wb_w", wb_w_raw)
@@ -222,9 +230,9 @@ def tile_list_xcross_noneP_kernel(tc, tab_words, tab_scales, wb_words, wb_scales
         first_product(D, 0, held="held1")
         second_product([A, B], 2)
         first_product(D, 1, held="held2")
-        for c in (A, B):
-            cross(c, 1)
-            store(c, 0, 2)
+        cross(A, 1)
+        cross(B, 1)
+        store_ab(0, 2)
         cross(C, 0)
         cross(C, 1)
         store(C, 0, 2)
@@ -238,11 +246,16 @@ def tile_list_xcross_noneP_kernel(tc, tab_words, tab_scales, wb_words, wb_scales
         bf_c = sbuf("bf_c", [P, CHUNK, PACK], BF16)
         bf_d = sbuf("bf_d", [P, CHUNK, PACK], BF16)
         woven = {A: bf_ab[:, span(A), :], B: bf_ab[:, span(B), :], C: bf_c[:]}
-        for c, t in ((A, 2), (B, 2), (A, 3), (B, 3), (C, 2), (C, 3)):
-            cross(c, t)
-            store(c, t, t + 1)
-            if t == PACK - 1:
-                weave(c, woven[c])
+        for t in (2, 3):
+            cross(A, t)
+            cross(B, t)
+            store_ab(t, t + 1)
+        weave(A, woven[A])
+        weave(B, woven[B])
+        cross(C, 2)
+        cross(C, 3)
+        store(C, 2, 4)
+        weave(C, woven[C])
         cross(D, 0)
         cross(D, 1)
         store(D, 0, 2)

@@ -34,23 +34,22 @@ def tile_list_xcross_noneP_kernel(tc, tab_words, tab_scales, wb_words, wb_scales
     with ExitStack() as ctx:
         keep = ctx.enter_context(tc.tile_pool(name="keep", bufs=1))
         psum = ctx.enter_context(tc.psum_pool(name="psum", bufs=8))
-
         shared = ctx.enter_context(tc.tile_pool(name="shared", bufs=1))
 
-        def sbuf(name, shape, dtype, tag=None):
-            if isinstance(tag, int):
-                return shared.tile(shape, dtype, name=name, align_bytes=64, offset=tag)
-            return keep.tile(shape, dtype, name=name, tag=tag or name, align_bytes=64)
+        def sbuf(name, shape, dtype, offset=None):
+            if offset is not None:
+                return shared.tile(shape, dtype, name=name, align_bytes=64, offset=offset)
+            return keep.tile(shape, dtype, name=name, tag=name, align_bytes=64)
 
         offsets = keep.tile([P, J // 16], U16, name="offsets")
         tab_s = sbuf("tab_s", [P, T], U8)
         tab_w = sbuf("tab_w", [P, T], I32)
-        dn_s_raw = sbuf("dn_s_raw", [P, R], U8, 5888)
-        wb_s_raw = sbuf("wb_s_raw", [P, N], U8, 4096)
+        dn_s_raw = sbuf("dn_s_raw", [P, R], U8, 2816)
+        wb_s_raw = sbuf("wb_s_raw", [P, N], U8, 448)
         dn_w_raw = sbuf("dn_w_raw", [P, 2 * R], U8)
         wb_w_raw = sbuf("wb_w_raw", [P, 2 * N], U8)
         up_cols = [slice(0, UP_SPLIT), slice(UP_SPLIT, N)]
-        up_raw = [sbuf("up_raw0", [P, PACK, UP_SPLIT], F32, 0), sbuf("up_raw1", [P, PACK, N - UP_SPLIT], F32)]
+        up_raw = [sbuf("up_raw0", [P, PACK, UP_SPLIT], F32, 5120), sbuf("up_raw1", [P, PACK, N - UP_SPLIT], F32, 10240)]
         bias = sbuf("bias", [P, PACK], F32)
         bias1 = sbuf("bias1", [P, PACK], F32)
         x0 = [sbuf("x0_%d" % t, [P, T], F32) for t in range(PACK)]
@@ -67,10 +66,10 @@ def tile_list_xcross_noneP_kernel(tc, tab_words, tab_scales, wb_words, wb_scales
         load_scale_rows(nc.sync, tab_s, tab_scales)
         nc.sync.dma_start(tab_w[:], tab_words[0].rearrange("p t i -> p (t i)").bitcast(I32))
         load_scale_rows(nc.sync, dn_s_raw, dn_scales)
+        nc.sync.dma_start(bias[:], b.rearrange("(p t) -> p t", t=PACK))
         for u in range(2):
             nc.sync.dma_start(up_raw[u][:], up_rows[:, :, up_cols[u]])
         load_scale_rows(nc.sync, wb_s_raw, wb_scales)
-        nc.sync.dma_start(bias[:], b.rearrange("(p t) -> p t", t=PACK))
         for t in range(PACK):
             nc.sync.dma_start(x0[t][:], x0_rows[:, t, :])
 
@@ -82,38 +81,47 @@ def tile_list_xcross_noneP_kernel(tc, tab_words, tab_scales, wb_words, wb_scales
             )
             return words
 
-        def deal_scales(name, raw, tag=None):
-            scales = sbuf(name, [P, N], U8, tag)
+        def deal_scales(name, raw):
+            scales = sbuf(name, [P, N], U8)
             nc.vector.tensor_copy(
                 scales[:].rearrange("p (t m) -> p t m", t=PACK),
                 raw[:].rearrange("p (m t) -> p t m", t=PACK),
             )
             return scales
 
-        def entries(c):
-            return offsets[:, c * CHUNK // 16 : (c + 1) * CHUNK // 16]
+        def entries(first, last):
+            return offsets[:, first // 16 : last // 16]
 
         def span(c):
             return slice(c * CHUNK, (c + 1) * CHUNK)
 
         A, B, C, D = range(J // CHUNK)
-        v_s = sbuf("v_s", [P, J], U8)
-        up_bf = sbuf("up_bf", [P, PACK * N], BF16)
+        v_s_all = sbuf("v_s_all", [P, J], U8)
+        v_w_a = sbuf("v_w_a", [P, CHUNK], U32)
+        v_w_bc = sbuf("v_w_bc", [P, 2 * CHUNK], U32, 1024)
+        up_bf = sbuf("up_bf", [P, PACK * N], BF16, 16384)
+        v_s = [v_s_all[:, span(c)] for c in (A, B, C, D)]
+        v_w = [v_w_a[:], v_w_bc[:, span(0)], v_w_bc[:, span(1)]]
         up_w = sbuf("up_w", [P, N], U32)
-        up_s = sbuf("up_s", [P, N], U8, 4352)
-        h_s = [sbuf("h_s%d" % c, [P, CHUNK], U8, 4096 if c == A else None) for c in (A, B, C, D)]
+        up_s = sbuf("up_s", [P, N], U8, 0)
+        h_bf_a = sbuf("h_bf_a", [P, CHUNK, PACK], BF16, 4096)
+        h_bf_bc = sbuf("h_bf_bc", [P, 2 * CHUNK, PACK], BF16, 6144)
+        h_bf_d = sbuf("h_bf_d", [P, CHUNK, PACK], BF16)
+        h_bf = [h_bf_a[:], h_bf_bc[:, span(0), :], h_bf_bc[:, span(1), :], h_bf_d[:]]
+        h_w = [sbuf("h_w%d" % c, [P, CHUNK], U32, at) for c, at in ((A, None), (B, None), (C, 20480), (D, 21504))]
+        h_s = [sbuf("h_s%d" % c, [P, CHUNK], U8, at) for c, at in ((A, 512), (B, 768), (C, None), (D, None))]
         o_w = sbuf("o_w", [P, J], I32)
         o_s = sbuf("o_s", [P, J], U8)
         res_ab = sbuf("res_ab", [P, PACK, 2 * CHUNK], F32)
         res_c = sbuf("res_c", [P, PACK, CHUNK], F32)
-        res_d = sbuf("res_d", [P, PACK, CHUNK], F32)
+        res_d = sbuf("res_d", [P, PACK, CHUNK], F32, 24576)
         res = [res_ab[:, :, span(A)], res_ab[:, :, span(B)], res_c[:], res_d[:]]
         out_rows = out_0.rearrange("(p t) j -> p t j", t=PACK)
         out_words = out_1[0].rearrange("p j i -> p (j i)").bitcast(I32)
-        v_w, h_bf, h_w, y1 = {}, {}, {}, {}
+        y1 = {}
 
         def new_bank(held):
-            return psum.tile([P, 2 * CHUNK], F32, name="bank", tag=held or "ring", bufs=1 if held else 6)[:]
+            return psum.tile([P, 2 * CHUNK], F32, name="bank", tag="held" if held else "ring", bufs=1 if held else 7)[:]
 
         def round_up(copy, u):
             copy(
@@ -121,13 +129,10 @@ def tile_list_xcross_noneP_kernel(tc, tab_words, tab_scales, wb_words, wb_scales
                 up_raw[u][:].rearrange("p i (m t) -> p m i t", t=PACK),
             )
 
-        def gather_words(c, tag=None):
-            v_w[c] = sbuf("v_w%d" % c, [P, CHUNK], U32, tag)
-            nc.vector.tensor_copy(v_w[c][:], tab_w[:].bitcast(U32).indirect(entries(c)))
+        def gather_words(c):
+            nc.vector.tensor_copy(v_w[c], tab_w[:].bitcast(U32).indirect(entries(c * CHUNK, (c + 1) * CHUNK)))
 
-        def first_product(c, piece, held=None):
-            if piece == 0:
-                h_bf[c] = sbuf("h_bf%d" % c, [P, CHUNK, PACK], BF16, 2048 * c if c in (A, B) else None)
+        def first_product(c, piece, held=False):
             cols = slice(piece * PASS_N, (piece + 1) * PASS_N)
             bank = new_bank(held).rearrange("p (t j) -> p t j", t=PACK)
             for t in range(PACK):
@@ -136,17 +141,21 @@ def tile_list_xcross_noneP_kernel(tc, tab_words, tab_scales, wb_words, wb_scales
                     lhsT=dn_w[:, 2 * P * t : 2 * P * (t + 1)].bitcast(FP4X4),
                     lhsT_scale=dn_s[:, P * t : P * (t + 1)],
                     rhs=v_w[c][:, cols].bitcast(FP8X4),
-                    rhs_scale=v_s[:, span(c)][:, cols],
+                    rhs_scale=v_s[c][:, cols],
                     start=True,
                     stop=True,
                 )
             nc.scalar.copy(h_bf[c][:, cols, :], bank.rearrange("p t j -> p j t"))
 
-        def quantise_h(c, tag=None):
-            h_w[c] = sbuf("h_w%d" % c, [P, CHUNK], U32, tag)
-            nc.vector.quantize_mx(out=h_w[c][:].bitcast(FP8X4), scales=h_s[c][:], in_=h_bf[c][:].rearrange("p j t -> p (j t)"))
+        def quantise_up(t0, t1):
+            nc.vector.quantize_mx(
+                out=up_w[:, P * t0 : P * t1].bitcast(FP8X4), scales=up_s[:, P * t0 : P * t1], in_=up_bf[:, N * t0 : N * t1]
+            )
 
-        def second_product(chunks, t, dest=None, held=None):
+        def quantise_h(c):
+            nc.vector.quantize_mx(out=h_w[c][:].bitcast(FP8X4), scales=h_s[c][:], in_=h_bf[c].rearrange("p j t -> p (j t)"))
+
+        def second_product(chunks, t, dest=None, offset=None, held=False):
             width = CHUNK * len(chunks)
             bank = new_bank(held)
             rows = slice(P * t, P * (t + 1))
@@ -168,19 +177,23 @@ def tile_list_xcross_noneP_kernel(tc, tab_words, tab_scales, wb_words, wb_scales
                         lhsT=wb_w[:, 2 * P * t : 2 * P * (t + 1)].bitcast(FP4X4),
                         lhsT_scale=wb_s[:, rows],
                         rhs=v_w[c][:, cols].bitcast(FP8X4),
-                        rhs_scale=v_s[:, span(c)][:, cols],
+                        rhs_scale=v_s[c][:, cols],
                         start=False,
                         stop=True,
                     )
             if dest is None:
-                dest = sbuf("y1_%d_%d" % (chunks[0], t), [P, width], F32)[:]
+                dest = sbuf("y1_%d_%d" % (chunks[0], t), [P, width], F32, offset)[:]
             nc.scalar.activation(dest, bank[:, :width], IDENT, bias=bias1[:, t : t + 1])
+            y1[tuple(chunks), t] = dest
             for n, c in enumerate(chunks):
-                y1[c, t] = dest[:, n * CHUNK : (n + 1) * CHUNK]
+                y1[(c,), t] = dest[:, n * CHUNK : (n + 1) * CHUNK]
 
         def cross(c, t, part=slice(0, CHUNK)):
-            picks = entries(c)[:, part.start // 16 : part.stop // 16]
-            nc.vector.tensor_tensor(res[c][:, t, part], x0[t][:].indirect(picks), y1[c, t][:, part], MULT)
+            picks = entries(c * CHUNK + part.start, c * CHUNK + part.stop)
+            nc.vector.tensor_tensor(res[c][:, t, part], x0[t][:].indirect(picks), y1[(c,), t][:, part], MULT)
+
+        def cross_ab(t):
+            nc.vector.tensor_tensor(res_ab[:, t, :], x0[t][:].indirect(entries(0, 2 * CHUNK)), y1[(A, B), t], MULT)
 
         def store(c, t0, t1):
             nc.sync.dma_start(out_rows[:, t0:t1, span(c)], res[c][:, t0:t1, :])
@@ -188,8 +201,8 @@ def tile_list_xcross_noneP_kernel(tc, tab_words, tab_scales, wb_words, wb_scales
         def store_ab(t0, t1):
             nc.sync.dma_start(out_rows[:, t0:t1, : 2 * CHUNK], res_ab[:, t0:t1, :])
 
-        def weave(c, dest, part=slice(0, CHUNK)):
-            nc.scalar.copy(dest[:, part, :].rearrange("p (c i) t -> p c t i", i=4), res[c][:, :, part].rearrange("p t (c i) -> p c t i", i=4))
+        def weave(c, dest, part=slice(0, CHUNK), copy=nc.scalar.copy):
+            copy(dest[:, part, :].rearrange("p (c i) t -> p c t i", i=4), res[c][:, :, part].rearrange("p t (c i) -> p c t i", i=4))
 
         def quantise_out(src, cols):
             nc.vector.quantize_mx(out=o_w[:, cols].bitcast(FP8X4), scales=o_s[:, cols], in_=src.rearrange("p j t -> p (j t)"))
@@ -200,73 +213,77 @@ def tile_list_xcross_noneP_kernel(tc, tab_words, tab_scales, wb_words, wb_scales
 
         dn_w = deal_words("dn_w", dn_w_raw)
         wb_w = deal_words("wb_w", wb_w_raw)
-        nc.vector.tensor_copy(v_s[:], tab_s[:].indirect(offsets[:]))
+        nc.vector.tensor_copy(v_s_all[:], tab_s[:].indirect(offsets[:]))
         gather_words(A)
         dn_s = deal_scales("dn_s", dn_s_raw)
-        gather_words(B, 5120)
-        gather_words(C, 6144)
+        gather_words(B)
+        gather_words(C)
+        nc.scalar.activation(bias1[:], bias[:], IDENT, bias=1.0)
         round_up(nc.scalar.copy, 0)
-        first_product(A, 0)
-        first_product(A, 1)
-        first_product(B, 0, held="held1")
-        first_product(B, 1, held="held2")
         round_up(nc.vector.tensor_copy, 1)
         wb_s = deal_scales("wb_s", wb_s_raw)
-        nc.vector.quantize_mx(out=up_w[:].bitcast(FP8X4), scales=up_s[:], in_=up_bf[:])
+        first_product(A, 0)
+        first_product(A, 1)
+        first_product(B, 0)
+        first_product(B, 1)
+        first_product(C, 0)
         quantise_h(A)
-        gather_words(D, 0)
+        quantise_up(0, 1)
+        quantise_up(1, 2)
+        quantise_up(2, 4)
         quantise_h(B)
-        first_product(C, 0, held="held1")
-        first_product(C, 1, held="held2")
-        quantise_h(C)
-        nc.scalar.activation(bias1[:], bias[:], IDENT, bias=1.0)
-        second_product([A], 0)
+        v_w.append(sbuf("v_w_d", [P, CHUNK], U32, 16384)[:])
+        gather_words(D)
+        second_product([A], 0, offset=20480, held=True)
         second_product([B], 0)
+        second_product([A], 1, offset=21504)
+        first_product(C, 1, held=True)
+        second_product([B], 1, offset=22528)
+        first_product(D, 0)
+        first_product(D, 1)
         cross(A, 0)
         cross(B, 0)
-        second_product([A, B], 1, flat(C)[:, : 2 * CHUNK])
-        second_product([C], 0, res[B][:, 2, :], held="held1")
-        second_product([C], 1, res[A][:, 2, :], held="held2")
-        first_product(D, 0, held="held1")
-        second_product([A, B], 2)
-        first_product(D, 1, held="held2")
+        quantise_h(C)
+        second_product([C], 0, offset=24576)
+        second_product([C], 1)
         cross(A, 1)
         cross(B, 1)
         store_ab(0, 2)
+        quantise_h(D)
         cross(C, 0)
         cross(C, 1)
         store(C, 0, 2)
-        quantise_h(D)
-        second_product([A, B], 3, flat(C)[:, 2 * CHUNK :])
-        second_product([C], 2, flat(D)[:, CHUNK // 2 : 3 * CHUNK // 2])
+        second_product([A, B], 2, offset=22528)
+        second_product([C], 2)
+        second_product([A, B], 3, flat(D)[:, : 2 * CHUNK])
         second_product([C], 3, res[D][:, 2, :])
+        cross_ab(2)
+        store_ab(2, 3)
+        cross(C, 2)
+        cross(A, 3)
+        cross(B, 3)
+        store_ab(3, 4)
         for t in range(PACK):
             second_product([D], t)
         bf_ab = sbuf("bf_ab", [P, 2 * CHUNK, PACK], BF16)
         bf_c = sbuf("bf_c", [P, CHUNK, PACK], BF16)
         bf_d = sbuf("bf_d", [P, CHUNK, PACK], BF16)
-        woven = {A: bf_ab[:, span(A), :], B: bf_ab[:, span(B), :], C: bf_c[:]}
-        for t in (2, 3):
-            cross(A, t)
-            cross(B, t)
-            store_ab(t, t + 1)
-        weave(A, woven[A])
-        weave(B, woven[B])
-        cross(C, 2)
+        weave(A, bf_ab[:, span(A), :])
+        weave(B, bf_ab[:, span(B), :])
         cross(C, 3)
         store(C, 2, 4)
-        weave(C, woven[C])
+        weave(C, bf_c[:])
         cross(D, 0)
         cross(D, 1)
         store(D, 0, 2)
         cross(D, 2)
         store(D, 2, 3)
         halves = [slice(0, CHUNK // 2), slice(CHUNK // 2, CHUNK)]
-        for part in halves:
-            cross(D, 3, part)
+        cross(D, 3, halves[1])
+        cross(D, 3, halves[0])
         store(D, 3, 4)
-        for part in halves:
-            weave(D, bf_d[:], part)
+        weave(D, bf_d[:], halves[1], nc.vector.tensor_copy)
+        weave(D, bf_d[:], halves[0])
         quantise_out(bf_ab[:], slice(0, 2 * CHUNK))
         quantise_out(bf_c[:], span(C))
         quantise_out(bf_d[:], span(D))

@@ -45,7 +45,8 @@ def tile_list_xcross_noneP_kernel(tc, tab_words, tab_scales, wb_words, wb_scales
         tab_s = sbuf("tab_s", [P, T], U8)
         tab_w = sbuf("tab_w", [P, T], I32)
         dn_s_raw = sbuf("dn_s_raw", [P, R], U8, 2816)
-        wb_s_raw = sbuf("wb_s_raw", [P, N], U8, 448)
+        scale_strip = sbuf("scale_strip", [P, 832], U8)
+        wb_s_raw = scale_strip[:, 256:768]
         dn_w_raw = sbuf("dn_w_raw", [P, 2 * R], U8)
         wb_w_raw = sbuf("wb_w_raw", [P, 2 * N], U8)
         up_cols = [slice(0, UP_SPLIT), slice(UP_SPLIT, N)]
@@ -55,7 +56,7 @@ def tile_list_xcross_noneP_kernel(tc, tab_words, tab_scales, wb_words, wb_scales
         x0 = [sbuf("x0_%d" % t, [P, T], F32) for t in range(PACK)]
 
         nc.gpsimd.memset(tab_s[:, : T // 2].bitcast(I32), 0)
-        for plane in (tab_s[:, T // 2 :], dn_s_raw[:], wb_s_raw[:]):
+        for plane in (tab_s[:, T // 2 :], dn_s_raw[:], wb_s_raw):
             nc.vector.memset(plane.bitcast(I32), 0)
 
         x0_rows = x0T.rearrange("(p t) c -> p t c", t=PACK)
@@ -103,16 +104,16 @@ def tile_list_xcross_noneP_kernel(tc, tab_words, tab_scales, wb_words, wb_scales
         v_s = [v_s_all[:, span(c)] for c in (A, B, C, D)]
         v_w = [v_w_a[:], v_w_bc[:, span(0)], v_w_bc[:, span(1)]]
         up_w = sbuf("up_w", [P, N], U32)
-        up_s = sbuf("up_s", [P, N], U8, 0)
+        up_s = scale_strip[:, 320:832]
         h_bf_a = sbuf("h_bf_a", [P, CHUNK, PACK], BF16, 4096)
         h_bf_bc = sbuf("h_bf_bc", [P, 2 * CHUNK, PACK], BF16, 6144)
         h_bf_d = sbuf("h_bf_d", [P, CHUNK, PACK], BF16)
         h_bf = [h_bf_a[:], h_bf_bc[:, span(0), :], h_bf_bc[:, span(1), :], h_bf_d[:]]
-        h_w = [sbuf("h_w%d" % c, [P, CHUNK], U32, at) for c, at in ((A, None), (B, None), (C, 20480), (D, 21504))]
-        h_s = [sbuf("h_s%d" % c, [P, CHUNK], U8, at) for c, at in ((A, 512), (B, 768), (C, None), (D, None))]
+        h_w = [sbuf("h_w%d" % c, [P, CHUNK], U32, at) for c, at in ((A, None), (B, 4096), (C, 20480), (D, 21504))]
+        h_s = [scale_strip[:, 64:320]] + [sbuf("h_s%d" % c, [P, CHUNK], U8)[:] for c in (B, C, D)]
         o_w = sbuf("o_w", [P, J], I32)
         o_s = sbuf("o_s", [P, J], U8)
-        res_ab = sbuf("res_ab", [P, PACK, 2 * CHUNK], F32)
+        res_ab = sbuf("res_ab", [P, PACK, 2 * CHUNK], F32, 32768)
         res_c = sbuf("res_c", [P, PACK, CHUNK], F32)
         res_d = sbuf("res_d", [P, PACK, CHUNK], F32, 24576)
         res = [res_ab[:, :, span(A)], res_ab[:, :, span(B)], res_c[:], res_d[:]]
@@ -153,34 +154,24 @@ def tile_list_xcross_noneP_kernel(tc, tab_words, tab_scales, wb_words, wb_scales
             )
 
         def quantise_h(c):
-            nc.vector.quantize_mx(out=h_w[c][:].bitcast(FP8X4), scales=h_s[c][:], in_=h_bf[c].rearrange("p j t -> p (j t)"))
+            nc.vector.quantize_mx(out=h_w[c][:].bitcast(FP8X4), scales=h_s[c], in_=h_bf[c].rearrange("p j t -> p (j t)"))
 
-        def second_product(chunks, t, dest=None, offset=None, held=False):
+        def second_product(chunks, t, dest=None, offset=None, held=False, wb_first=False):
             width = CHUNK * len(chunks)
             bank = new_bank(held)
             rows = slice(P * t, P * (t + 1))
+            passes = []
             for n, c in enumerate(chunks):
-                for piece in range(CHUNK // PASS_N):
-                    cols = slice(piece * PASS_N, (piece + 1) * PASS_N)
-                    sums = bank[:, n * CHUNK : (n + 1) * CHUNK][:, cols]
-                    nc.tensor.matmul_mx(
-                        out=sums,
-                        lhsT=up_w[:, rows].bitcast(FP8X4),
-                        lhsT_scale=up_s[:, rows],
-                        rhs=h_w[c][:, cols].bitcast(FP8X4),
-                        rhs_scale=h_s[c][:, cols],
-                        start=True,
-                        stop=False,
-                    )
-                    nc.tensor.matmul_mx(
-                        out=sums,
-                        lhsT=wb_w[:, 2 * P * t : 2 * P * (t + 1)].bitcast(FP4X4),
-                        lhsT_scale=wb_s[:, rows],
-                        rhs=v_w[c][:, cols].bitcast(FP8X4),
-                        rhs_scale=v_s[c][:, cols],
-                        start=False,
-                        stop=True,
-                    )
+                up_pass = (bank[:, span(n)], up_w[:, rows].bitcast(FP8X4), up_s[:, rows], h_w[c][:], h_s[c])
+                wb_passes = [
+                    (bank[:, span(n)][:, cols], wb_w[:, 2 * P * t : 2 * P * (t + 1)].bitcast(FP4X4), wb_s[:, rows], v_w[c][:, cols], v_s[c][:, cols])
+                    for cols in (slice(0, PASS_N), slice(PASS_N, CHUNK))
+                ]
+                passes.extend(wb_passes + [up_pass] if wb_first else [up_pass] + wb_passes)
+            for n, (sums, lhs, lhs_scale, rhs, rhs_scale) in enumerate(passes):
+                nc.tensor.matmul_mx(
+                    out=sums, lhsT=lhs, lhsT_scale=lhs_scale, rhs=rhs.bitcast(FP8X4), rhs_scale=rhs_scale, start=n == 0, stop=n == len(passes) - 1
+                )
             if dest is None:
                 dest = sbuf("y1_%d_%d" % (chunks[0], t), [P, width], F32, offset)[:]
             nc.scalar.activation(dest, bank[:, :width], IDENT, bias=bias1[:, t : t + 1])
@@ -206,7 +197,6 @@ def tile_list_xcross_noneP_kernel(tc, tab_words, tab_scales, wb_words, wb_scales
 
         def quantise_out(src, cols):
             nc.vector.quantize_mx(out=o_w[:, cols].bitcast(FP8X4), scales=o_s[:, cols], in_=src.rearrange("p j t -> p (j t)"))
-            nc.sync.dma_start(out_words[:, cols], o_w[:, cols])
 
         def flat(c):
             return res[c].rearrange("p t j -> p (t j)")
@@ -216,25 +206,30 @@ def tile_list_xcross_noneP_kernel(tc, tab_words, tab_scales, wb_words, wb_scales
         nc.vector.tensor_copy(v_s_all[:], tab_s[:].indirect(offsets[:]))
         gather_words(A)
         dn_s = deal_scales("dn_s", dn_s_raw)
+        nc.vector.tensor_scalar_add(bias1[:], bias[:], 1.0)
         gather_words(B)
         gather_words(C)
-        nc.scalar.activation(bias1[:], bias[:], IDENT, bias=1.0)
         round_up(nc.scalar.copy, 0)
         round_up(nc.vector.tensor_copy, 1)
-        wb_s = deal_scales("wb_s", wb_s_raw)
+        wb_s = sbuf("wb_s", [P, N], U8)
+        for part in (slice(0, 48), slice(48, P)):
+            nc.vector.tensor_copy(
+                wb_s[:].rearrange("p (t m) -> p t m", t=PACK)[:, :, part],
+                wb_s_raw.rearrange("p (m t) -> p t m", t=PACK)[:, :, part],
+            )
         first_product(A, 0)
         first_product(A, 1)
         first_product(B, 0)
         first_product(B, 1)
         first_product(C, 0)
-        quantise_h(A)
         quantise_up(0, 1)
+        quantise_h(A)
         quantise_up(1, 2)
         quantise_up(2, 4)
         quantise_h(B)
         v_w.append(sbuf("v_w_d", [P, CHUNK], U32, 16384)[:])
         gather_words(D)
-        second_product([A], 0, offset=20480, held=True)
+        second_product([A], 0, offset=20480, held=True, wb_first=True)
         second_product([B], 0)
         second_product([A], 1, offset=21504)
         first_product(C, 1, held=True)
@@ -267,7 +262,7 @@ def tile_list_xcross_noneP_kernel(tc, tab_words, tab_scales, wb_words, wb_scales
             second_product([D], t)
         bf_ab = sbuf("bf_ab", [P, 2 * CHUNK, PACK], BF16)
         bf_c = sbuf("bf_c", [P, CHUNK, PACK], BF16)
-        bf_d = sbuf("bf_d", [P, CHUNK, PACK], BF16)
+        bf_d = sbuf("bf_d", [P, CHUNK, PACK], BF16, 32768)
         weave(A, bf_ab[:, span(A), :])
         weave(B, bf_ab[:, span(B), :])
         cross(C, 3)
@@ -282,11 +277,14 @@ def tile_list_xcross_noneP_kernel(tc, tab_words, tab_scales, wb_words, wb_scales
         cross(D, 3, halves[1])
         cross(D, 3, halves[0])
         store(D, 3, 4)
+        quantise_out(bf_ab[:], slice(0, 2 * CHUNK))
+        nc.sync.dma_start(out_words[:, : 2 * CHUNK], o_w[:, : 2 * CHUNK])
         weave(D, bf_d[:], halves[1], nc.vector.tensor_copy)
         weave(D, bf_d[:], halves[0])
-        quantise_out(bf_ab[:], slice(0, 2 * CHUNK))
         quantise_out(bf_c[:], span(C))
+        nc.sync.dma_start(out_words[:, span(C)], o_w[:, span(C)])
         quantise_out(bf_d[:], span(D))
+        nc.sync.dma_start(out_words[:, span(D)], o_w[:, span(D)])
         for r in range(4):
             queue = nc.sync if r % 2 == 0 else nc.scalar
             queue.dma_start(out_2[0, r:16:4, :].bitcast(I32), o_s[r:P:32, :].bitcast(I32))

@@ -206,9 +206,9 @@ def tile_list_xcross_noneP_kernel(tc, tab_words, tab_scales, wb_words, wb_scales
         nc.vector.tensor_copy(v_s_all[:], tab_s[:].indirect(offsets[:]))
         gather_words(A)
         dn_s = deal_scales("dn_s", dn_s_raw)
-        nc.vector.tensor_scalar_add(bias1[:], bias[:], 1.0)
         gather_words(B)
         gather_words(C)
+        nc.scalar.activation(bias1[:], bias[:], IDENT, bias=1.0)
         round_up(nc.scalar.copy, 0)
         round_up(nc.vector.tensor_copy, 1)
         wb_s = sbuf("wb_s", [P, N], U8)

@@ -21,7 +21,7 @@ P = 128
 PACK = 4
 PASS_N = 128
 CHUNK = 256
-UP_SPLIT = 192
+UP_SPLIT = 128
 
 
 def load_scale_rows(queue, plane, scales):
@@ -50,7 +50,7 @@ def tile_list_xcross_noneP_kernel(tc, tab_words, tab_scales, wb_words, wb_scales
         dn_w_raw = sbuf("dn_w_raw", [P, 2 * R], U8)
         wb_w_raw = sbuf("wb_w_raw", [P, 2 * N], U8)
         up_cols = [slice(0, UP_SPLIT), slice(UP_SPLIT, N)]
-        up_raw = [sbuf("up_raw0", [P, PACK, UP_SPLIT], F32, 5120), sbuf("up_raw1", [P, PACK, N - UP_SPLIT], F32, 10240)]
+        up_raw = [sbuf("up_raw0", [P, PACK, UP_SPLIT], F32, 5120), sbuf("up_raw1", [P, PACK, N - UP_SPLIT], F32)]
         bias = sbuf("bias", [P, PACK], F32)
         bias1 = sbuf("bias1", [P, PACK], F32)
         x0 = [sbuf("x0_%d" % t, [P, T], F32) for t in range(PACK)]
@@ -106,23 +106,34 @@ def tile_list_xcross_noneP_kernel(tc, tab_words, tab_scales, wb_words, wb_scales
         up_w = sbuf("up_w", [P, N], U32)
         up_s = scale_strip[:, 320:832]
         h_bf_a = sbuf("h_bf_a", [P, CHUNK, PACK], BF16, 4096)
-        h_bf_bc = sbuf("h_bf_bc", [P, 2 * CHUNK, PACK], BF16, 6144)
+        h_bf_bc = sbuf("h_bf_bc", [P, CHUNK + PASS_N, PACK], BF16, 6144)
+        h_bf_c1 = sbuf("h_bf_c1", [P, PASS_N, PACK], BF16, 30720)
         h_bf_d = sbuf("h_bf_d", [P, CHUNK, PACK], BF16)
-        h_bf = [h_bf_a[:], h_bf_bc[:, span(0), :], h_bf_bc[:, span(1), :], h_bf_d[:]]
-        h_w = [sbuf("h_w%d" % c, [P, CHUNK], U32, at) for c, at in ((A, None), (B, 4096), (C, 20480), (D, 21504))]
+        h_bf = {
+            (A, 0): h_bf_a[:, :PASS_N, :],
+            (A, 1): h_bf_a[:, PASS_N:, :],
+            (B, 0): h_bf_bc[:, :PASS_N, :],
+            (B, 1): h_bf_bc[:, PASS_N:CHUNK, :],
+            (C, 0): h_bf_bc[:, CHUNK:, :],
+            (C, 1): h_bf_c1[:],
+            (D, 0): h_bf_d[:, :PASS_N, :],
+            (D, 1): h_bf_d[:, PASS_N:, :],
+        }
+        h_whole = {A: h_bf_a[:], B: h_bf_bc[:, :CHUNK, :], D: h_bf_d[:]}
+        h_w = [sbuf("h_w%d" % c, [P, CHUNK], U32, at) for c, at in ((A, None), (B, 4096), (C, 20480), (D, 44544))]
         h_s = [scale_strip[:, 64:320]] + [sbuf("h_s%d" % c, [P, CHUNK], U8)[:] for c in (B, C, D)]
         o_w = sbuf("o_w", [P, J], I32)
         o_s = sbuf("o_s", [P, J], U8)
         res_ab = sbuf("res_ab", [P, PACK, 2 * CHUNK], F32, 32768)
-        res_c = sbuf("res_c", [P, PACK, CHUNK], F32)
+        res_c = sbuf("res_c", [P, PACK, CHUNK], F32, 45568)
         res_d = sbuf("res_d", [P, PACK, CHUNK], F32, 24576)
         res = [res_ab[:, :, span(A)], res_ab[:, :, span(B)], res_c[:], res_d[:]]
         out_rows = out_0.rearrange("(p t) j -> p t j", t=PACK)
         out_words = out_1[0].rearrange("p j i -> p (j i)").bitcast(I32)
         y1 = {}
 
-        def new_bank(held):
-            return psum.tile([P, 2 * CHUNK], F32, name="bank", tag="held" if held else "ring", bufs=1 if held else 7)[:]
+        def new_bank():
+            return psum.tile([P, 2 * CHUNK], F32, name="bank")[:]
 
         def round_up(copy, u):
             copy(
@@ -133,9 +144,9 @@ def tile_list_xcross_noneP_kernel(tc, tab_words, tab_scales, wb_words, wb_scales
         def gather_words(c):
             nc.vector.tensor_copy(v_w[c], tab_w[:].bitcast(U32).indirect(entries(c * CHUNK, (c + 1) * CHUNK)))
 
-        def first_product(c, piece, held=False):
+        def first_product(c, piece):
             cols = slice(piece * PASS_N, (piece + 1) * PASS_N)
-            bank = new_bank(held).rearrange("p (t j) -> p t j", t=PACK)
+            bank = new_bank().rearrange("p (t j) -> p t j", t=PACK)
             for t in range(PACK):
                 nc.tensor.matmul_mx(
                     out=bank[:, t, :],
@@ -146,7 +157,7 @@ def tile_list_xcross_noneP_kernel(tc, tab_words, tab_scales, wb_words, wb_scales
                     start=True,
                     stop=True,
                 )
-            nc.scalar.copy(h_bf[c][:, cols, :], bank.rearrange("p t j -> p j t"))
+            nc.scalar.copy(h_bf[c, piece], bank.rearrange("p t j -> p j t"))
 
         def quantise_up(t0, t1):
             nc.vector.quantize_mx(
@@ -154,11 +165,15 @@ def tile_list_xcross_noneP_kernel(tc, tab_words, tab_scales, wb_words, wb_scales
             )
 
         def quantise_h(c):
-            nc.vector.quantize_mx(out=h_w[c][:].bitcast(FP8X4), scales=h_s[c], in_=h_bf[c].rearrange("p j t -> p (j t)"))
+            nc.vector.quantize_mx(out=h_w[c][:].bitcast(FP8X4), scales=h_s[c], in_=h_whole[c].rearrange("p j t -> p (j t)"))
 
-        def second_product(chunks, t, dest=None, offset=None, held=False, wb_first=False):
+        def quantise_h_piece(c, piece):
+            cols = slice(piece * PASS_N, (piece + 1) * PASS_N)
+            nc.vector.quantize_mx(out=h_w[c][:, cols].bitcast(FP8X4), scales=h_s[c][:, cols], in_=h_bf[c, piece].rearrange("p j t -> p (j t)"))
+
+        def second_product(chunks, t, dest=None, offset=None, wb_first=False, column=None):
             width = CHUNK * len(chunks)
-            bank = new_bank(held)
+            bank = new_bank()
             rows = slice(P * t, P * (t + 1))
             passes = []
             for n, c in enumerate(chunks):
@@ -174,7 +189,7 @@ def tile_list_xcross_noneP_kernel(tc, tab_words, tab_scales, wb_words, wb_scales
                 )
             if dest is None:
                 dest = sbuf("y1_%d_%d" % (chunks[0], t), [P, width], F32, offset)[:]
-            nc.scalar.activation(dest, bank[:, :width], IDENT, bias=bias1[:, t : t + 1])
+            nc.scalar.activation(dest, bank[:, :width], IDENT, bias=bias1[:, t : t + 1] if column is None else column)
             y1[tuple(chunks), t] = dest
             for n, c in enumerate(chunks):
                 y1[(c,), t] = dest[:, n * CHUNK : (n + 1) * CHUNK]
@@ -204,11 +219,24 @@ def tile_list_xcross_noneP_kernel(tc, tab_words, tab_scales, wb_words, wb_scales
         dn_w = deal_words("dn_w", dn_w_raw)
         wb_w = deal_words("wb_w", wb_w_raw)
         nc.vector.tensor_copy(v_s_all[:], tab_s[:].indirect(offsets[:]))
+        warm = new_bank()
+        for half in range(2):
+            nc.tensor.matmul_mx(
+                out=warm,
+                lhsT=dn_w[:, : 2 * P].bitcast(FP4X4),
+                lhsT_scale=tab_s[:, :P],
+                rhs=tab_w[:, half * 2 * CHUNK : (half + 1) * 2 * CHUNK].bitcast(FP8X4),
+                rhs_scale=tab_s[:, half * 2 * CHUNK : (half + 1) * 2 * CHUNK],
+                start=True,
+                stop=True,
+            )
         gather_words(A)
         dn_s = deal_scales("dn_s", dn_s_raw)
         gather_words(B)
         gather_words(C)
         nc.scalar.activation(bias1[:], bias[:], IDENT, bias=1.0)
+        bias1_first = sbuf("bias1_first", [P, 1], F32, 30720)
+        nc.scalar.activation(bias1_first[:], bias[:, 0:1], IDENT, bias=1.0)
         round_up(nc.scalar.copy, 0)
         round_up(nc.vector.tensor_copy, 1)
         wb_s = sbuf("wb_s", [P, N], U8)
@@ -229,16 +257,17 @@ def tile_list_xcross_noneP_kernel(tc, tab_words, tab_scales, wb_words, wb_scales
         quantise_h(B)
         v_w.append(sbuf("v_w_d", [P, CHUNK], U32, 16384)[:])
         gather_words(D)
-        second_product([A], 0, offset=20480, held=True, wb_first=True)
+        second_product([A], 0, offset=20480, wb_first=True, column=bias1_first[:])
         second_product([B], 0)
-        second_product([A], 1, offset=21504)
-        first_product(C, 1, held=True)
+        second_product([A], 1, offset=45056)
+        first_product(C, 1)
         second_product([B], 1, offset=22528)
         first_product(D, 0)
         first_product(D, 1)
         cross(A, 0)
         cross(B, 0)
-        quantise_h(C)
+        quantise_h_piece(C, 0)
+        quantise_h_piece(C, 1)
         second_product([C], 0, offset=24576)
         second_product([C], 1)
         cross(A, 1)

@@ -55,8 +55,7 @@ def tile_list_xcross_noneP_kernel(tc, tab_words, tab_scales, wb_words, wb_scales
         bias1 = sbuf("bias1", [P, PACK], F32)
         x0 = [sbuf("x0_%d" % t, [P, T], F32) for t in range(PACK)]
 
-        nc.gpsimd.memset(tab_s[:, : T // 2].bitcast(I32), 0)
-        for plane in (tab_s[:, T // 2 :], dn_s_raw[:], wb_s_raw):
+        for plane in (tab_s[:], dn_s_raw[:], wb_s_raw):
             nc.vector.memset(plane.bitcast(I32), 0)
 
         x0_rows = x0T.rearrange("(p t) c -> p t c", t=PACK)

@@ -218,17 +218,6 @@ def tile_list_xcross_noneP_kernel(tc, tab_words, tab_scales, wb_words, wb_scales
         dn_w = deal_words("dn_w", dn_w_raw)
         wb_w = deal_words("wb_w", wb_w_raw)
         nc.vector.tensor_copy(v_s_all[:], tab_s[:].indirect(offsets[:]))
-        warm = new_bank()
-        for half in range(2):
-            nc.tensor.matmul_mx(
-                out=warm,
-                lhsT=dn_w[:, : 2 * P].bitcast(FP4X4),
-                lhsT_scale=tab_s[:, :P],
-                rhs=tab_w[:, half * 2 * CHUNK : (half + 1) * 2 * CHUNK].bitcast(FP8X4),
-                rhs_scale=tab_s[:, half * 2 * CHUNK : (half + 1) * 2 * CHUNK],
-                start=True,
-                stop=True,
-            )
         gather_words(A)
         dn_s = deal_scales("dn_s", dn_s_raw)
         gather_words(B)

@@ -21,7 +21,8 @@ P = 128
 PACK = 4
 PASS_N = 128
 CHUNK = 256
-UP_SPLIT = 128
+UP_SPLIT = 192
+LAST = 96
 
 
 def load_scale_rows(queue, plane, scales):
@@ -290,9 +291,9 @@ def tile_list_xcross_noneP_kernel(tc, tab_words, tab_scales, wb_words, wb_scales
         store(D, 0, 2)
         cross(D, 2)
         store(D, 2, 3)
-        halves = [slice(0, CHUNK // 2), slice(CHUNK // 2, CHUNK)]
-        cross(D, 3, halves[1])
-        cross(D, 3, halves[0])
+        halves = [slice(0, CHUNK - LAST), slice(CHUNK - LAST, CHUNK)]
+        for part in halves:
+            cross(D, 3, part)
         store(D, 3, 4)
         quantise_out(bf_ab[:], slice(0, 2 * CHUNK))
         nc.sync.dma_start(out_words[:, : 2 * CHUNK], o_w[:, : 2 * CHUNK])

@@ -45,14 +45,14 @@ def tile_list_xcross_noneP_kernel(tc, tab_words, tab_scales, wb_words, wb_scales
         offsets = keep.tile([P, J // 16], U16, name="offsets")
         tab_s = sbuf("tab_s", [P, T], U8)
         tab_w = sbuf("tab_w", [P, T], I32)
-        dn_s_raw = sbuf("dn_s_raw", [P, R], U8, 2816)
+        dn_s_raw = sbuf("dn_s_raw", [P, R], U8)
         scale_strip = sbuf("scale_strip", [P, 832], U8)
         wb_s_raw = scale_strip[:, 256:768]
         dn_w_raw = sbuf("dn_w_raw", [P, 2 * R], U8)
         wb_w_raw = sbuf("wb_w_raw", [P, 2 * N], U8)
         up_cols = [slice(0, UP_SPLIT), slice(UP_SPLIT, N)]
         up_raw = [sbuf("up_raw0", [P, PACK, UP_SPLIT], F32, 5120), sbuf("up_raw1", [P, PACK, N - UP_SPLIT], F32)]
-        bias = sbuf("bias", [P, PACK], F32)
+        bias = sbuf("bias", [P, PACK], F32, 2816)
         bias1 = sbuf("bias1", [P, PACK], F32)
         x0 = [sbuf("x0_%d" % t, [P, T], F32) for t in range(PACK)]
 
@@ -98,11 +98,11 @@ def tile_list_xcross_noneP_kernel(tc, tab_words, tab_scales, wb_words, wb_scales
 
         A, B, C, D = range(J // CHUNK)
         v_s_all = sbuf("v_s_all", [P, J], U8)
-        v_w_a = sbuf("v_w_a", [P, CHUNK], U32)
-        v_w_bc = sbuf("v_w_bc", [P, 2 * CHUNK], U32, 1024)
+        v_w_first = sbuf("v_w_first", [P, PASS_N], U32)
+        v_w_rest = sbuf("v_w_rest", [P, PASS_N + 2 * CHUNK], U32, 512)
         up_bf = sbuf("up_bf", [P, PACK * N], BF16, 16384)
         v_s = [v_s_all[:, span(c)] for c in (A, B, C, D)]
-        v_w = [v_w_a[:], v_w_bc[:, span(0)], v_w_bc[:, span(1)]]
+        v_w = [v_w_first[:]] + [v_w_rest[:, n * PASS_N : (n + 1) * PASS_N] for n in range(5)]
         up_w = sbuf("up_w", [P, N], U32)
         up_s = scale_strip[:, 320:832]
         h_bf_a = sbuf("h_bf_a", [P, CHUNK, PACK], BF16, 4096)
@@ -141,8 +141,8 @@ def tile_list_xcross_noneP_kernel(tc, tab_words, tab_scales, wb_words, wb_scales
                 up_raw[u][:].rearrange("p i (m t) -> p m i t", t=PACK),
             )
 
-        def gather_words(c):
-            nc.vector.tensor_copy(v_w[c], tab_w[:].bitcast(U32).indirect(entries(c * CHUNK, (c + 1) * CHUNK)))
+        def gather_words(dest, first):
+            nc.vector.tensor_copy(dest, tab_w[:].bitcast(U32).indirect(entries(first, first + dest.shape[1])))
 
         def first_product(c, piece):
             cols = slice(piece * PASS_N, (piece + 1) * PASS_N)
@@ -152,7 +152,7 @@ def tile_list_xcross_noneP_kernel(tc, tab_words, tab_scales, wb_words, wb_scales
                     out=bank[:, t, :],
                     lhsT=dn_w[:, 2 * P * t : 2 * P * (t + 1)].bitcast(FP4X4),
                     lhsT_scale=dn_s[:, P * t : P * (t + 1)],
-                    rhs=v_w[c][:, cols].bitcast(FP8X4),
+                    rhs=v_w[2 * c + piece].bitcast(FP8X4),
                     rhs_scale=v_s[c][:, cols],
                     start=True,
                     stop=True,
@@ -179,8 +179,8 @@ def tile_list_xcross_noneP_kernel(tc, tab_words, tab_scales, wb_words, wb_scales
             for n, c in enumerate(chunks):
                 up_pass = (bank[:, span(n)], up_w[:, rows].bitcast(FP8X4), up_s[:, rows], h_w[c][:], h_s[c])
                 wb_passes = [
-                    (bank[:, span(n)][:, cols], wb_w[:, 2 * P * t : 2 * P * (t + 1)].bitcast(FP4X4), wb_s[:, rows], v_w[c][:, cols], v_s[c][:, cols])
-                    for cols in (slice(0, PASS_N), slice(PASS_N, CHUNK))
+                    (bank[:, span(n)][:, cols], wb_w[:, 2 * P * t : 2 * P * (t + 1)].bitcast(FP4X4), wb_s[:, rows], v_w[2 * c + piece], v_s[c][:, cols])
+                    for piece, cols in enumerate((slice(0, PASS_N), slice(PASS_N, CHUNK)))
                 ]
                 passes.extend(wb_passes + [up_pass] if wb_first else [up_pass] + wb_passes)
             for n, (sums, lhs, lhs_scale, rhs, rhs_scale) in enumerate(passes):
@@ -219,13 +219,14 @@ def tile_list_xcross_noneP_kernel(tc, tab_words, tab_scales, wb_words, wb_scales
         dn_w = deal_words("dn_w", dn_w_raw)
         wb_w = deal_words("wb_w", wb_w_raw)
         nc.vector.tensor_copy(v_s_all[:], tab_s[:].indirect(offsets[:]))
-        gather_words(A)
+        gather_words(v_w_first[:], 0)
         dn_s = deal_scales("dn_s", dn_s_raw)
-        gather_words(B)
-        gather_words(C)
         nc.scalar.activation(bias1[:], bias[:], IDENT, bias=1.0)
         bias1_first = sbuf("bias1_first", [P, 1], F32, 30720)
-        nc.scalar.activation(bias1_first[:], bias[:, 0:1], IDENT, bias=1.0)
+        nc.scalar.copy(bias1_first[:], bias1[:, 0:1])
+        gather_words(v_w_rest[:, :PASS_N], PASS_N)
+        gather_words(v_w_rest[:, PASS_N : PASS_N + CHUNK], B * CHUNK)
+        gather_words(v_w_rest[:, PASS_N + CHUNK :], C * CHUNK)
         round_up(nc.scalar.copy, 0)
         round_up(nc.vector.tensor_copy, 1)
         wb_s = sbuf("wb_s", [P, N], U8)
@@ -244,8 +245,9 @@ def tile_list_xcross_noneP_kernel(tc, tab_words, tab_scales, wb_words, wb_scales
         quantise_up(1, 2)
         quantise_up(2, 4)
         quantise_h(B)
-        v_w.append(sbuf("v_w_d", [P, CHUNK], U32, 16384)[:])
-        gather_words(D)
+        v_w_d = sbuf("v_w_d", [P, CHUNK], U32, 16384)
+        v_w.extend([v_w_d[:, :PASS_N], v_w_d[:, PASS_N:]])
+        gather_words(v_w_d[:], D * CHUNK)
         second_product([A], 0, offset=20480, wb_first=True, column=bias1_first[:])
         second_product([B], 0)
         second_product([A], 1, offset=45056)

@@ -106,20 +106,19 @@ def tile_list_xcross_noneP_kernel(tc, tab_words, tab_scales, wb_words, wb_scales
         up_w = sbuf("up_w", [P, N], U32)
         up_s = scale_strip[:, 320:832]
         h_bf_a = sbuf("h_bf_a", [P, CHUNK, PACK], BF16, 4096)
-        h_bf_bc = sbuf("h_bf_bc", [P, CHUNK + PASS_N, PACK], BF16, 6144)
-        h_bf_c1 = sbuf("h_bf_c1", [P, PASS_N, PACK], BF16, 30720)
+        h_bf_bc = sbuf("h_bf_bc", [P, 2 * CHUNK, PACK], BF16, 6144)
         h_bf_d = sbuf("h_bf_d", [P, CHUNK, PACK], BF16)
         h_bf = {
             (A, 0): h_bf_a[:, :PASS_N, :],
             (A, 1): h_bf_a[:, PASS_N:, :],
             (B, 0): h_bf_bc[:, :PASS_N, :],
             (B, 1): h_bf_bc[:, PASS_N:CHUNK, :],
-            (C, 0): h_bf_bc[:, CHUNK:, :],
-            (C, 1): h_bf_c1[:],
+            (C, 0): h_bf_bc[:, CHUNK : CHUNK + PASS_N, :],
+            (C, 1): h_bf_bc[:, CHUNK + PASS_N :, :],
             (D, 0): h_bf_d[:, :PASS_N, :],
             (D, 1): h_bf_d[:, PASS_N:, :],
         }
-        h_whole = {A: h_bf_a[:], B: h_bf_bc[:, :CHUNK, :], D: h_bf_d[:]}
+        h_whole = {A: h_bf_a[:], B: h_bf_bc[:, :CHUNK, :], C: h_bf_bc[:, CHUNK:, :], D: h_bf_d[:]}
         h_w = [sbuf("h_w%d" % c, [P, CHUNK], U32, at) for c, at in ((A, None), (B, 4096), (C, 20480), (D, 44544))]
         h_s = [scale_strip[:, 64:320]] + [sbuf("h_s%d" % c, [P, CHUNK], U8)[:] for c in (B, C, D)]
         o_w = sbuf("o_w", [P, J], I32)
@@ -166,10 +165,6 @@ def tile_list_xcross_noneP_kernel(tc, tab_words, tab_scales, wb_words, wb_scales
 
         def quantise_h(c):
             nc.vector.quantize_mx(out=h_w[c][:].bitcast(FP8X4), scales=h_s[c], in_=h_whole[c].rearrange("p j t -> p (j t)"))
-
-        def quantise_h_piece(c, piece):
-            cols = slice(piece * PASS_N, (piece + 1) * PASS_N)
-            nc.vector.quantize_mx(out=h_w[c][:, cols].bitcast(FP8X4), scales=h_s[c][:, cols], in_=h_bf[c, piece].rearrange("p j t -> p (j t)"))
 
         def second_product(chunks, t, dest=None, offset=None, wb_first=False, column=None):
             width = CHUNK * len(chunks)
@@ -222,12 +217,12 @@ def tile_list_xcross_noneP_kernel(tc, tab_words, tab_scales, wb_words, wb_scales
         gather_words(v_w_first[:], 0)
         dn_s = deal_scales("dn_s", dn_s_raw)
         nc.scalar.activation(bias1[:], bias[:], IDENT, bias=1.0)
-        bias1_first = sbuf("bias1_first", [P, 1], F32, 30720)
-        nc.scalar.copy(bias1_first[:], bias1[:, 0:1])
         gather_words(v_w_rest[:, :PASS_N], PASS_N)
         gather_words(v_w_rest[:, PASS_N : PASS_N + CHUNK], B * CHUNK)
         gather_words(v_w_rest[:, PASS_N + CHUNK :], C * CHUNK)
         round_up(nc.scalar.copy, 0)
+        bias1_first = h_bf_bc[:, 2 * CHUNK - 1, 0:2].bitcast(F32)
+        nc.scalar.copy(bias1_first, bias1[:, 0:1])
         round_up(nc.vector.tensor_copy, 1)
         wb_s = sbuf("wb_s", [P, N], U8)
         for part in (slice(0, 48), slice(48, P)):
@@ -242,23 +237,21 @@ def tile_list_xcross_noneP_kernel(tc, tab_words, tab_scales, wb_words, wb_scales
         first_product(C, 0)
         quantise_up(0, 1)
         quantise_h(A)
-        quantise_up(1, 2)
-        quantise_up(2, 4)
+        quantise_up(1, 4)
         quantise_h(B)
         v_w_d = sbuf("v_w_d", [P, CHUNK], U32, 16384)
         v_w.extend([v_w_d[:, :PASS_N], v_w_d[:, PASS_N:]])
         gather_words(v_w_d[:], D * CHUNK)
-        second_product([A], 0, offset=20480, wb_first=True, column=bias1_first[:])
+        second_product([A], 0, offset=20480, wb_first=True, column=bias1_first)
         second_product([B], 0)
-        second_product([A], 1, offset=45056)
         first_product(C, 1)
+        second_product([A], 1, offset=45056)
         second_product([B], 1, offset=22528)
         first_product(D, 0)
         first_product(D, 1)
         cross(A, 0)
         cross(B, 0)
-        quantise_h_piece(C, 0)
-        quantise_h_piece(C, 1)
+        quantise_h(C)
         second_product([C], 0, offset=24576)
         second_product([C], 1)
         cross(A, 1)
@@ -269,16 +262,16 @@ def tile_list_xcross_noneP_kernel(tc, tab_words, tab_scales, wb_words, wb_scales
         cross(C, 1)
         store(C, 0, 2)
         second_product([A, B], 2, offset=22528)
-        second_product([C], 2)
+        second_product([C, D], 2)
         second_product([A, B], 3, flat(D)[:, : 2 * CHUNK])
-        second_product([C], 3, res[D][:, 2, :])
+        second_product([D, C], 3, flat(D)[:, 2 * CHUNK :])
         cross_ab(2)
         store_ab(2, 3)
         cross(C, 2)
         cross(A, 3)
         cross(B, 3)
         store_ab(3, 4)
-        for t in range(PACK):
+        for t in range(2):
             second_product([D], t)
         bf_ab = sbuf("bf_ab", [P, 2 * CHUNK, PACK], BF16)
         bf_c = sbuf("bf_c", [P, CHUNK, PACK], BF16)
@@ -289,14 +282,14 @@ def tile_list_xcross_noneP_kernel(tc, tab_words, tab_scales, wb_words, wb_scales
         store(C, 2, 4)
         weave(C, bf_c[:])
         cross(D, 0)
+        cross(D, 3)
+        store(D, 3, 4)
         cross(D, 1)
         store(D, 0, 2)
-        cross(D, 2)
-        store(D, 2, 3)
         halves = [slice(0, CHUNK - LAST), slice(CHUNK - LAST, CHUNK)]
         for part in halves:
-            cross(D, 3, part)
-        store(D, 3, 4)
+            cross(D, 2, part)
+        store(D, 2, 3)
         quantise_out(bf_ab[:], slice(0, 2 * CHUNK))
         nc.sync.dma_start(out_words[:, : 2 * CHUNK], o_w[:, : 2 * CHUNK])
         weave(D, bf_d[:], halves[1], nc.vector.tensor_copy)

@@ -268,6 +268,7 @@ def tile_list_xcross_noneP_kernel(tc, tab_words, tab_scales, wb_words, wb_scales
         cross_ab(2)
         store_ab(2, 3)
         cross(C, 2)
+        store(C, 2, 3)
         cross(A, 3)
         cross(B, 3)
         store_ab(3, 4)
@@ -279,13 +280,14 @@ def tile_list_xcross_noneP_kernel(tc, tab_words, tab_scales, wb_words, wb_scales
         weave(A, bf_ab[:, span(A), :])
         weave(B, bf_ab[:, span(B), :])
         cross(C, 3)
-        store(C, 2, 4)
+        store(C, 3, 4)
         weave(C, bf_c[:])
         cross(D, 0)
+        store(D, 0, 1)
         cross(D, 3)
         store(D, 3, 4)
         cross(D, 1)
-        store(D, 0, 2)
+        store(D, 1, 2)
         halves = [slice(0, CHUNK - LAST), slice(CHUNK - LAST, CHUNK)]
         for part in halves:
             cross(D, 2, part)

from contextlib import ExitStack

import concourse.mybir as mybir

K, R, N, T, J = 512, 512, 512, 2048, 1024
FLOPS = 2 * J * (K * R + K * N + R * N)

F32 = mybir.dt.float32
BF16 = mybir.dt.bfloat16
I32 = mybir.dt.int32
U32 = mybir.dt.uint32
U16 = mybir.dt.uint16
U8 = mybir.dt.uint8
FP8X4 = mybir.dt.float8_e4m3fn_x4
FP4X4 = mybir.dt.float4_e2m1fn_x4
MULT = mybir.AluOpType.mult
ADD = mybir.AluOpType.add
IDENT = mybir.ActivationFunctionType.Identity

P = 128
PACK = 4
PASS_N = 128
CHUNK = 256
UP_SPLIT = 192
LAST = 96


def load_scale_rows(queue, plane, scales):
    for r in range(4):
        queue.dma_start(plane[r:P:32, :].bitcast(I32), scales[0, r:16:4, :].bitcast(I32))


def tile_list_xcross_noneP_kernel(tc, tab_words, tab_scales, wb_words, wb_scales, dn_words, dn_scales, upw, x0T, b, offs, out_0, out_1, out_2):
    nc = tc.nc
    with ExitStack() as ctx:
        keep = ctx.enter_context(tc.tile_pool(name="keep", bufs=1))
        psum = ctx.enter_context(tc.psum_pool(name="psum", bufs=8))
        shared = ctx.enter_context(tc.tile_pool(name="shared", bufs=1))

        def sbuf(name, shape, dtype, offset=None):
            if offset is not None:
                return shared.tile(shape, dtype, name=name, align_bytes=64, offset=offset)
            return keep.tile(shape, dtype, name=name, tag=name, align_bytes=64)

        offsets = keep.tile([P, J // 16], U16, name="offsets")
        tab_s = sbuf("tab_s", [P, T], U8)
        tab_w = sbuf("tab_w", [P, T], I32)
        dn_s_raw = sbuf("dn_s_raw", [P, R], U8)
        scale_strip = sbuf("scale_strip", [P, 832], U8)
        wb_s_raw = scale_strip[:, 256:768]
        dn_w_raw = sbuf("dn_w_raw", [P, 2 * R], U8)
        wb_w_raw = sbuf("wb_w_raw", [P, 2 * N], U8)
        up_cols = [slice(0, UP_SPLIT), slice(UP_SPLIT, N)]
        up_raw = [sbuf("up_raw0", [P, PACK, UP_SPLIT], F32, 5120), sbuf("up_raw1", [P, PACK, N - UP_SPLIT], F32)]
        bias = sbuf("bias", [P, PACK], F32, 2816)
        bias1 = sbuf("bias1", [P, PACK], F32)
        x0 = [sbuf("x0_%d" % t, [P, T], F32) for t in range(PACK)]

        for plane in (tab_s[:], dn_s_raw[:], wb_s_raw):
            nc.vector.memset(plane.bitcast(I32), 0)

        x0_rows = x0T.rearrange("(p t) c -> p t c", t=PACK)
        up_rows = upw.rearrange("(p i) n -> p i n", i=PACK)
        nc.sync.dma_start(dn_w_raw[:].bitcast(I32), dn_words[0].bitcast(I32))
        nc.sync.dma_start(wb_w_raw[:].bitcast(I32), wb_words[0].bitcast(I32))
        nc.sync.dma_start(offsets[:], offs)
        load_scale_rows(nc.sync, tab_s, tab_scales)
        nc.sync.dma_start(tab_w[:], tab_words[0].rearrange("p t i -> p (t i)").bitcast(I32))
        load_scale_rows(nc.sync, dn_s_raw, dn_scales)
        nc.sync.dma_start(bias[:], b.rearrange("(p t) -> p t", t=PACK))
        for u in range(2):
            nc.sync.dma_start(up_raw[u][:], up_rows[:, :, up_cols[u]])
        load_scale_rows(nc.sync, wb_s_raw, wb_scales)
        for t in range(PACK):
            nc.sync.dma_start(x0[t][:], x0_rows[:, t, :])

        def deal_words(name, raw):
            words = sbuf(name, [P, 2 * N], U8)
            nc.vector.tensor_copy(
                words[:].bitcast(U16).rearrange("p (t m) -> p t m", t=PACK),
                raw[:].bitcast(U16).rearrange("p (m t) -> p t m", t=PACK),
            )
            return words

        def deal_scales(name, raw):
            scales = sbuf(name, [P, N], U8)
            nc.vector.tensor_copy(
                scales[:].rearrange("p (t m) -> p t m", t=PACK),
                raw[:].rearrange("p (m t) -> p t m", t=PACK),
            )
            return scales

        def entries(first, last):
            return offsets[:, first // 16 : last // 16]

        def span(c):
            return slice(c * CHUNK, (c + 1) * CHUNK)

        A, B, C, D = range(J // CHUNK)
        v_s_all = sbuf("v_s_all", [P, J], U8)
        v_w_first = sbuf("v_w_first", [P, PASS_N], U32)
        v_w_rest = sbuf("v_w_rest", [P, PASS_N + 2 * CHUNK], U32, 512)
        up_bf = sbuf("up_bf", [P, PACK * N], BF16, 16384)
        v_s = [v_s_all[:, span(c)] for c in (A, B, C, D)]
        v_w = [v_w_first[:]] + [v_w_rest[:, n * PASS_N : (n + 1) * PASS_N] for n in range(5)]
        up_w = sbuf("up_w", [P, N], U32)
        up_s = scale_strip[:, 320:832]
        h_bf_a = sbuf("h_bf_a", [P, CHUNK, PACK], BF16, 4096)
        h_bf_bc = sbuf("h_bf_bc", [P, 2 * CHUNK, PACK], BF16, 6144)
        h_bf_d = sbuf("h_bf_d", [P, CHUNK, PACK], BF16)
        h_bf = {
            (A, 0): h_bf_a[:, :PASS_N, :],
            (A, 1): h_bf_a[:, PASS_N:, :],
            (B, 0): h_bf_bc[:, :PASS_N, :],
            (B, 1): h_bf_bc[:, PASS_N:CHUNK, :],
            (C, 0): h_bf_bc[:, CHUNK : CHUNK + PASS_N, :],
            (C, 1): h_bf_bc[:, CHUNK + PASS_N :, :],
            (D, 0): h_bf_d[:, :PASS_N, :],
            (D, 1): h_bf_d[:, PASS_N:, :],
        }
        h_whole = {A: h_bf_a[:], B: h_bf_bc[:, :CHUNK, :], C: h_bf_bc[:, CHUNK:, :], D: h_bf_d[:]}
        h_w = [sbuf("h_w%d" % c, [P, CHUNK], U32, at) for c, at in ((A, None), (B, 4096), (C, 20480), (D, 44544))]
        h_s = [scale_strip[:, 64:320]] + [sbuf("h_s%d" % c, [P, CHUNK], U8)[:] for c in (B, C, D)]
        o_w = sbuf("o_w", [P, J], I32)
        o_s = sbuf("o_s", [P, J], U8)
        res_ab = sbuf("res_ab", [P, PACK, 2 * CHUNK], F32, 32768)
        res_c = sbuf("res_c", [P, PACK, CHUNK], F32, 45568)
        res_d = sbuf("res_d", [P, PACK, CHUNK], F32, 24576)
        res = [res_ab[:, :, span(A)], res_ab[:, :, span(B)], res_c[:], res_d[:]]
        out_rows = out_0.rearrange("(p t) j -> p t j", t=PACK)
        out_words = out_1[0].rearrange("p j i -> p (j i)").bitcast(I32)
        y1 = {}

        def new_bank():
            return psum.tile([P, 2 * CHUNK], F32, name="bank")[:]

        def round_up(copy, u):
            copy(
                up_bf[:].rearrange("p (t m i) -> p m i t", t=PACK, i=PACK)[:, up_cols[u].start // PACK : up_cols[u].stop // PACK],
                up_raw[u][:].rearrange("p i (m t) -> p m i t", t=PACK),
            )

        def gather_words(dest, first):
            nc.vector.tensor_copy(dest, tab_w[:].bitcast(U32).indirect(entries(first, first + dest.shape[1])))

        def first_product(c, piece):
            cols = slice(piece * PASS_N, (piece + 1) * PASS_N)
            bank = new_bank().rearrange("p (t j) -> p t j", t=PACK)
            for t in range(PACK):
                nc.tensor.matmul_mx(
                    out=bank[:, t, :],
                    lhsT=dn_w[:, 2 * P * t : 2 * P * (t + 1)].bitcast(FP4X4),
                    lhsT_scale=dn_s[:, P * t : P * (t + 1)],
                    rhs=v_w[2 * c + piece].bitcast(FP8X4),
                    rhs_scale=v_s[c][:, cols],
                    start=True,
                    stop=True,
                )
            nc.scalar.copy(h_bf[c, piece], bank.rearrange("p t j -> p j t"))

        def quantise_up(t0, t1):
            nc.vector.quantize_mx(
                out=up_w[:, P * t0 : P * t1].bitcast(FP8X4), scales=up_s[:, P * t0 : P * t1], in_=up_bf[:, N * t0 : N * t1]
            )

        def quantise_h(c):
            nc.vector.quantize_mx(out=h_w[c][:].bitcast(FP8X4), scales=h_s[c], in_=h_whole[c].rearrange("p j t -> p (j t)"))

        def second_product(chunks, t, dest=None, offset=None, wb_first=False, column=None):
            width = CHUNK * len(chunks)
            bank = new_bank()
            rows = slice(P * t, P * (t + 1))
            passes = []
            for n, c in enumerate(chunks):
                up_pass = (bank[:, span(n)], up_w[:, rows].bitcast(FP8X4), up_s[:, rows], h_w[c][:], h_s[c])
                wb_passes = [
                    (bank[:, span(n)][:, cols], wb_w[:, 2 * P * t : 2 * P * (t + 1)].bitcast(FP4X4), wb_s[:, rows], v_w[2 * c + piece], v_s[c][:, cols])
                    for piece, cols in enumerate((slice(0, PASS_N), slice(PASS_N, CHUNK)))
                ]
                passes.extend(wb_passes + [up_pass] if wb_first else [up_pass] + wb_passes)
            for n, (sums, lhs, lhs_scale, rhs, rhs_scale) in enumerate(passes):
                nc.tensor.matmul_mx(
                    out=sums, lhsT=lhs, lhsT_scale=lhs_scale, rhs=rhs.bitcast(FP8X4), rhs_scale=rhs_scale, start=n == 0, stop=n == len(passes) - 1
                )
            if dest is None:
                dest = sbuf("y1_%d_%d" % (chunks[0], t), [P, width], F32, offset)[:]
            nc.scalar.activation(dest, bank[:, :width], IDENT, bias=bias1[:, t : t + 1] if column is None else column)
            y1[tuple(chunks), t] = dest
            for n, c in enumerate(chunks):
                y1[(c,), t] = dest[:, n * CHUNK : (n + 1) * CHUNK]

        def cross(c, t, part=slice(0, CHUNK)):
            picks = entries(c * CHUNK + part.start, c * CHUNK + part.stop)
            nc.vector.tensor_tensor(res[c][:, t, part], x0[t][:].indirect(picks), y1[(c,), t][:, part], MULT)

        def cross_ab(t):
            nc.vector.tensor_tensor(res_ab[:, t, :], x0[t][:].indirect(entries(0, 2 * CHUNK)), y1[(A, B), t], MULT)

        def store(c, t0, t1):
            nc.sync.dma_start(out_rows[:, t0:t1, span(c)], res[c][:, t0:t1, :])

        def store_ab(t0, t1):
            nc.sync.dma_start(out_rows[:, t0:t1, : 2 * CHUNK], res_ab[:, t0:t1, :])

        def weave(c, dest, part=slice(0, CHUNK), copy=nc.scalar.copy):
            copy(dest[:, part, :].rearrange("p (c i) t -> p c t i", i=4), res[c][:, :, part].rearrange("p t (c i) -> p c t i", i=4))

        def quantise_out(src, cols):
            nc.vector.quantize_mx(out=o_w[:, cols].bitcast(FP8X4), scales=o_s[:, cols], in_=src.rearrange("p j t -> p (j t)"))

        def flat(c):
            return res[c].rearrange("p t j -> p (t j)")

        dn_w = deal_words("dn_w", dn_w_raw)
        wb_w = deal_words("wb_w", wb_w_raw)
        nc.vector.tensor_copy(v_s_all[:], tab_s[:].indirect(offsets[:]))
        gather_words(v_w_first[:], 0)
        dn_s = deal_scales("dn_s", dn_s_raw)
        nc.scalar.activation(bias1[:], bias[:], IDENT, bias=1.0)
        gather_words(v_w_rest[:, :PASS_N], PASS_N)
        gather_words(v_w_rest[:, PASS_N : PASS_N + CHUNK], B * CHUNK)
        gather_words(v_w_rest[:, PASS_N + CHUNK :], C * CHUNK)
        round_up(nc.scalar.copy, 0)
        bias1_first = h_bf_bc[:, 2 * CHUNK - 1, 0:2].bitcast(F32)
        nc.scalar.copy(bias1_first, bias1[:, 0:1])
        round_up(nc.vector.tensor_copy, 1)
        wb_s = sbuf("wb_s", [P, N], U8)
        for part in (slice(0, 48), slice(48, P)):
            nc.vector.tensor_copy(
                wb_s[:].rearrange("p (t m) -> p t m", t=PACK)[:, :, part],
                wb_s_raw.rearrange("p (m t) -> p t m", t=PACK)[:, :, part],
            )
        first_product(A, 0)
        first_product(A, 1)
        first_product(B, 0)
        first_product(B, 1)
        first_product(C, 0)
        quantise_up(0, 1)
        quantise_h(A)
        quantise_up(1, 4)
        quantise_h(B)
        v_w_d = sbuf("v_w_d", [P, CHUNK], U32, 16384)
        v_w.extend([v_w_d[:, :PASS_N], v_w_d[:, PASS_N:]])
        gather_words(v_w_d[:], D * CHUNK)
        second_product([A], 0, offset=20480, wb_first=True, column=bias1_first)
        second_product([B], 0)
        first_product(C, 1)
        second_product([A], 1, offset=45056)
        second_product([B], 1, offset=22528)
        first_product(D, 0)
        first_product(D, 1)
        cross(A, 0)
        cross(B, 0)
        quantise_h(C)
        second_product([C], 0, offset=24576)
        second_product([C], 1)
        cross(A, 1)
        cross(B, 1)
        store_ab(0, 2)
        quantise_h(D)
        cross(C, 0)
        cross(C, 1)
        store(C, 0, 2)
        second_product([A, B], 2, offset=22528)
        second_product([C, D], 2)
        second_product([A, B], 3, flat(D)[:, : 2 * CHUNK])
        second_product([D, C], 3, flat(D)[:, 2 * CHUNK :])
        cross_ab(2)
        store_ab(2, 3)
        cross(C, 2)
        store(C, 2, 3)
        cross(A, 3)
        cross(B, 3)
        store_ab(3, 4)
        for t in range(2):
            second_product([D], t)
        bf_ab = sbuf("bf_ab", [P, 2 * CHUNK, PACK], BF16)
        bf_c = sbuf("bf_c", [P, CHUNK, PACK], BF16)
        bf_d = sbuf("bf_d", [P, CHUNK, PACK], BF16, 32768)
        weave(A, bf_ab[:, span(A), :])
        weave(B, bf_ab[:, span(B), :])
        cross(C, 3)
        store(C, 3, 4)
        weave(C, bf_c[:])
        cross(D, 0)
        store(D, 0, 1)
        cross(D, 3)
        store(D, 3, 4)
        cross(D, 1)
        store(D, 1, 2)
        halves = [slice(0, CHUNK - LAST), slice(CHUNK - LAST, CHUNK)]
        for part in halves:
            cross(D, 2, part)
        store(D, 2, 3)
        quantise_out(bf_ab[:], slice(0, 2 * CHUNK))
        nc.sync.dma_start(out_words[:, : 2 * CHUNK], o_w[:, : 2 * CHUNK])
        weave(D, bf_d[:], halves[1], nc.vector.tensor_copy)
        weave(D, bf_d[:], halves[0])
        quantise_out(bf_c[:], span(C))
        nc.sync.dma_start(out_words[:, span(C)], o_w[:, span(C)])
        quantise_out(bf_d[:], span(D))
        nc.sync.dma_start(out_words[:, span(D)], o_w[:, span(D)])
        for r in range(4):
            queue = nc.sync if r % 2 == 0 else nc.scalar
            queue.dma_start(out_2[0, r:16:4, :].bitcast(I32), o_s[r:P:32, :].bitcast(I32))
